import numpy as np, ml_dtypes
CORES = [2,3,42,43,82,83,122,123]
N = 8
import mx_ref
BF = ml_dtypes.bfloat16
def entries(a):
    return np.ascontiguousarray(a.T).reshape(-1)
def table(e):
    return np.ascontiguousarray(np.reshape(e, (-1, 16)).T).astype(np.int32)
def tile(rs):
    return np.stack(rs, axis=2).reshape(128, -1).astype(BF)
def cut(t, i, w=512):
    return t[:, w * i:w * i + w]
def f(rng, *shape):
    return mx_ref.flush((rng.standard_normal(shape, dtype=np.float32) * np.exp2(rng.integers(-2, 3, shape[:-1] + (1,)))).astype(BF))
def wide(rng, *shape, cols=0):
    v = rng.standard_normal(shape, dtype=np.float32) * np.exp2(rng.integers(-12, 13, shape)).astype(np.float32)
    if cols: v *= np.repeat(np.exp2(rng.integers(-cols, cols + 1, shape[:-2] + (1, shape[-1] // 4))) * (rng.random(shape[:-2] + (1, shape[-1] // 4)) > 0.0625), 4, axis=-1).astype(np.float32)
    return mx_ref.flush(v.astype(BF))
T, TG, C1, C2 = 512, 256, 320, 64
def layer(rng, C, M, own=0.25, full=False, hub=False, neg=None):
    snd = np.full((N, N, C), -1); src = np.zeros((N, M, 4), int)
    for s in range(N):
        for r in range(N):
            if s != r and own < 1:
                n = C if full else rng.integers(1, C + 1)
                snd[s, r, rng.permutation(C)[:n]] = rng.choice(T, n, replace=False)
    h, k, c = rng.integers(0, N), rng.integers(0, T), rng.integers(0, C, N)
    if hub:
        for r in range(N):
            if r != h: snd[h, r, c[r]] = k
    for r in range(N):
        src[r] = rng.integers(0, T, (M, 4))
        if own < 1:
            far = T + np.flatnonzero(snd[:, r].reshape(-1) >= 0)
            src[r] = np.where(rng.random((M, 4)) < own, src[r], rng.choice(far, (M, 4)))
        if hub:
            e = k if r == h else T + h * C + c[r]
            src[r][:, 0] = e; src[r][rng.permutation(M)[:M // 4]] = e
            src[r] = rng.permuted(src[r], axis=1)
        if neg is not None:
            bad = np.flatnonzero(np.concatenate([neg[r]] + [(snd[s, r] >= 0) & neg[s][snd[s, r]] for s in range(N)]))
            src[r][rng.permutation(M)[:M // 2]] = rng.choice(bad, (M // 2, 4))
    return np.stack([table(a) for a in snd]), np.stack([table(a) for a in src])
def lists(rng, neg=None, **o):
    a, b = layer(rng, C1, T, neg=neg, **o); c, e = layer(rng, C2, TG, **o)
    return {"snd1": a, "src1": b, "snd2": c, "src2": e}
def setup_inputs(rng):
    return {"x": f(rng, N, 128, 4 * T), "w1": np.repeat(f(rng, 1, 128, 4 * 512), N, axis=0), "w2": np.repeat(f(rng, 1, 128, 512), N, axis=0), **lists(rng)}
def setup_inputs_foreign(rng):
    return {**setup_inputs(rng), **lists(rng, own=0, full=True)}
def setup_inputs_hub(rng):
    return {**setup_inputs(rng), **lists(rng, hub=True)}
def setup_inputs_negative(rng):
    d = setup_inputs(rng)
    neg = np.stack([rng.permutation(T) < T // 2 for r in range(N)])
    v = np.abs(d["x"]).reshape(N, 128, T, 4)
    d["x"] = np.where(neg[:, None, :, None], -v, v).reshape(N, 128, 4 * T)
    d["w1"] = np.abs(d["w1"])
    return {**d, **lists(rng, neg=neg)}
def setup_inputs_self(rng):
    return {**setup_inputs(rng), **lists(rng, own=1)}
def setup_inputs_spread(rng):
    d = setup_inputs(rng); d["x"] = wide(rng, N, 128, 4 * T); return d
def check_inputs(d):
    b = []
    for k in ("w1", "w2"):
        if any(d[k][r].tobytes() != d[k][0].tobytes() for r in range(N)): b.append(k)
    for l, C in (("1", C1), ("2", C2)):
        snd = np.stack([entries(a) for a in d["snd" + l]]).reshape(N, N, C)
        if snd.min() < -1 or snd.max() >= T: b.append("snd" + l)
        for r in range(N):
            if (snd[r, r] != -1).any(): b.append("snd" + l)
            ok = np.concatenate([np.ones(T, bool), snd[:, r].reshape(-1) >= 0])
            e = entries(d["src" + l][r])
            if e.min() < 0 or e.max() >= T + N * C or not ok[e].all(): b.append("src" + l)
    return b
def most(v, snd, src, r, C):
    a = np.concatenate([v[r]] + [v[s][:, entries(snd[s])[r * C:r * C + C]] for s in range(N)], axis=1)
    return a[:, entries(src[r])].reshape(128, -1, 4).max(axis=2)
def reference(x, w1, w2, snd1, src1, snd2, src2):
    q = [mx_ref.quantize(x[r]) for r in range(N)]
    Z = [[mx_ref.matmul(mx_ref.quantize(cut(w1[r], i)), q[r]) for r in range(N)] for i in range(4)]
    U = []
    for r in range(N):
        h = tile([np.maximum(most(Z[i], snd1, src1, r, C1), np.float32(0)) * np.float32(0.05) for i in range(4)])
        U.append(mx_ref.matmul(mx_ref.quantize(w2[r]), mx_ref.quantize(h)))
    return {"y": np.stack([most(U, snd2, src2, r, C2) for r in range(N)])}

@@ -1,0 +1,457 @@
+from concourse.bass import DstId, RemoteDMATransfer
+from concourse.mybir import dt, AluOpType, ActivationFunctionType
+
+N = 8
+SIM_CORES = 128
+NODES, TARGETS, C1, C2 = 512, 256, 320, 64
+W = NODES + N * C1
+U = NODES + N * C2
+S1W, S2W = N * C1 // 16, N * C2 // 16
+R1W, R2W = 4 * NODES // 16, 4 * TARGETS // 16
+E1, E2 = NODES // 16, TARGETS // 16
+EW = E1 + E2
+MXC, MXS = "float8_e4m3fn_x4", "uint8"
+
+SCRATCH = {
+    "xs": ("sbuf", [128, 4 * NODES], "bfloat16"),
+    "w1s": ("sbuf", [128, 4 * 512], "bfloat16"),
+    "w2s": ("sbuf", [128, 4 * 128], "bfloat16"),
+    "lsa": ("sbuf", [128, S1W], "int32"),
+    "lsb": ("sbuf", [128, S2W], "int32"),
+    "lra": ("sbuf", [128, R1W], "int32"),
+    "lrb": ("sbuf", [16, R2W], "int32"),
+    "osa": ("sbuf", [128, 4 * S1W], "uint16"),
+    "osb": ("sbuf", [128, S2W], "uint16"),
+    "osc": ("sbuf", [128, S2W], "uint16"),
+    "ora": ("sbuf", [128, R1W], "uint16"),
+    "ecol": ("sbuf", [128, 4 * EW], "uint16"),
+    "erow": ("dram", [16, 4 * EW], "uint16"),
+    "ore": ("sbuf", [128, 4 * EW], "uint16"),
+    "xg": ("sbuf", [128, 4 * N * C1], "bfloat16"),
+    "xsc": ("sbuf", [128, N * C1], MXC), "xss": ("sbuf", [128, N * C1], MXS),
+    "xoc": ("sbuf", [128, NODES], MXC), "xos": ("sbuf", [128, NODES], MXS),
+    "xrc": ("sbuf", [128, N * C1], MXC), "xrs": ("sbuf", [128, N * C1], MXS),
+    "w1c": ("sbuf", [128, 512], MXC), "w1p": ("sbuf", [128, 512], MXS),
+    "w2c": ("sbuf", [128, 128], MXC), "w2p": ("sbuf", [128, 128], MXS),
+    "tb0": ("sbuf", [128, W], "bfloat16"), "tb1": ("sbuf", [128, W], "bfloat16"),
+    "tb2": ("sbuf", [128, W], "bfloat16"), "tb3": ("sbuf", [128, W], "bfloat16"),
+    "gg0": ("sbuf", [128, 3 * NODES], "bfloat16"), "gg1": ("sbuf", [128, 3 * NODES], "bfloat16"),
+    "gg2": ("sbuf", [128, 4 * NODES], "bfloat16"), "gg3": ("sbuf", [128, 4 * NODES], "bfloat16"),
+    "sc2": ("sbuf", [128, 4 * NODES], "bfloat16"), "sc3": ("sbuf", [128, 4 * NODES], "bfloat16"),
+    "mk": ("sbuf", [128, 4 * NODES], "bfloat16"),
+    "r0": ("sbuf", [128, NODES], "bfloat16"), "r1": ("sbuf", [128, NODES], "bfloat16"),
+    "ht": ("sbuf", [128, 4 * NODES], "bfloat16"),
+    "hg": ("sbuf", [128, 4 * N * C2], "bfloat16"),
+    "hsc": ("sbuf", [128, N * C2], MXC), "hss": ("sbuf", [128, N * C2], MXS),
+    "hoc": ("sbuf", [128, NODES + C2], MXC), "hos": ("sbuf", [128, NODES + C2], MXS),
+    "hrc": ("sbuf", [128, N * C2], MXC), "hrs": ("sbuf", [128, N * C2], MXS),
+    "ut": ("sbuf", [128, U], "float32"),
+    "g2": ("sbuf", [128, 3 * TARGETS], "float32"),
+    "yo": ("sbuf", [128, TARGETS], "float32"),
+    "f1c": ("sbuf", [128, 2 * C1], MXC), "f1s": ("sbuf", [128, 2 * C1], MXS),
+    "f2c": ("sbuf", [128, 2 * C2], MXC), "f2s": ("sbuf", [128, 2 * C2], MXS),
+    "pp": ("psum", [128, 512 * 8], "float32"),
+}
+SEMAPHORES = (["v", "s", "t", "loc", "dx", "dw1", "dw2", "dsa", "dsb", "dra", "drb", "der", "dre", "dy"]
+              + ["fc1a", "fs1a", "fc1b", "fs1b", "fc2", "fs2"]
+              + ["x%d" % r for r in range(N)] + ["h%d" % r for r in range(N)])
+
+MATE, DIE, DIRECT, OWN = "mate", "die", "direct", "own"
+
+PLAN = (("send", MATE, 0), ("self", None, 0), ("send", DIE, 0), ("hold", OWN, 0), ("send", MATE, 1), ("send", DIE, 1),
+        ("send", DIRECT, 0), ("rows", None, 0), ("take", None, 0), ("send", DIRECT, 1), ("take", OWN, 0), ("lists", None, 0),
+        ("take", MATE, 0), ("take", DIE, 0), ("take", DIRECT, 0), ("take", MATE, 1), ("take", DIE, 1), ("take", DIRECT, 1))
+
+
+def layout(T, topo):
+    chips, ranks = [], {}
+    for r, c in enumerate(T.cores):
+        ch = topo.chip(c)
+        if ch not in ranks:
+            chips.append(ch)
+            ranks[ch] = []
+        ranks[ch].append(r)
+    roads = {}
+    for ia, a in enumerate(chips):
+        for ib, b in enumerate(chips):
+            if a == b:
+                roads[a, b] = (OWN, None)
+                continue
+            src, dst = T.cores[ranks[a][0]], T.cores[ranks[b][0]]
+            k = len(ranks[a])
+            if topo.same_plane(a, b):
+                mid = [c for c in topo.cores_of(src) if topo.die(c) != topo.die(src) and topo.may_write(c, dst)
+                       and T.rank_of(c) is None]
+                roads[a, b] = (DIE, mid[:k])
+            elif (ib - ia) % len(chips) == 1:
+                roads[a, b] = (DIRECT, None)
+            else:
+                mid = [c for c in range(SIM_CORES) if topo.mates(topo.chip(c), b) and topo.die(c) == topo.die(dst)
+                       and topo.may_write(c, dst) and topo.may_write(src, c) and T.rank_of(c) is None]
+                roads[a, b] = (MATE, mid[:k])
+    return chips, ranks, roads
+
+
+def bits(engines):
+    m = 0
+    for e in engines:
+        m |= 1 << e
+    return m
+
+
+def u8(view):
+    return view.bitcast(dt.uint8)
+
+
+def firsts(k, n):
+    return [(k + i) % n for i in range(n)]
+
+
+def send_engines(src, dst, T, topo):
+    e = topo.engines(src, dst)
+    if topo.chip(src) != topo.chip(dst):
+        return e
+    far = [c for c in T.cores if topo.chip(c) != topo.chip(src)][0]
+    off = topo.engines(src, far)
+    return [k for k in e if k not in off]
+
+
+def hand_on(g, core, T, topo):
+    chips, ranks, roads = layout(T, topo)
+    for (a, b), (road, mid) in roads.items():
+        if not mid or core not in mid:
+            continue
+        k = mid.index(core)
+        s = ranks[a][k]
+        n = len(ranks[b])
+        w = len(send_engines(T.cores[s], core, T, topo))
+        sent = 0
+        for h, d in enumerate(firsts(k, n)):
+            dst = T.cores[ranks[b][d]]
+            rid, pid, _ = topo.addr(dst)
+            eng = topo.engines(core, dst)
+            arr = T.sem["x%d" % s]
+            g.wait_ge(T.sem["fc1" + "ab"[h]], w)
+            g.remote_dma(u8(T.xrc[:, s * C1:(s + 1) * C1]), u8(T.f1c[:, d * C1:(d + 1) * C1]), arr, T.sem.loc, pid, rid, bits(eng))
+            g.wait_ge(T.sem["fs1" + "ab"[h]], w)
+            g.remote_dma(T.xrs[:, s * C1:(s + 1) * C1], T.f1s[:, d * C1:(d + 1) * C1], arr, T.sem.loc, pid, rid, bits(eng))
+            sent += 2 * len(eng)
+        for sem, out, buf in (("fc2", "hrc", "f2c"), ("fs2", "hrs", "f2s")):
+            tr = []
+            for d in range(n):
+                dst = T.cores[ranks[b][d]]
+                rid, pid, _ = topo.addr(dst)
+                eng = topo.engines(core, dst)
+                e = len(eng) // n
+                o, i = T[out][:, s * C2:(s + 1) * C2], T[buf][:, d * C2:(d + 1) * C2]
+                if out == "hrc":
+                    o, i = u8(o), u8(i)
+                tr.append(RemoteDMATransfer(dst_ids=[DstId(rid=rid, pnc=pid)], dma_engine_mask=bits(eng[e * d:e * d + e]),
+                                            remote_sem=T.sem["h%d" % s], src=i, dst=o))
+                sent += e
+            g.wait_ge(T.sem[sem], w)
+            g.remote_dma_fused(tr, local_sem=T.sem.loc)
+        g.wait_ge(T.sem.loc, sent)
+
+
+def join(runs):
+    out = []
+    for a, b in sorted(runs):
+        if out and out[-1][1] == a:
+            out[-1] = (out[-1][0], b)
+        else:
+            out.append((a, b))
+    return out
+
+
+def rank_program(g, core, T, topo):
+    rank = T.rank_of(core)
+    if rank is None:
+        hand_on(g, core, T, topo)
+        return
+    chips, ranks, roads = layout(T, topo)
+    me = topo.chip(core)
+    mine = ranks[me].index(rank)
+    near = [r for r in ranks[me] if r != rank]
+    goes = {roads[me, b][0]: b for b in chips}
+    came = {roads[a, me][0]: a for a in chips}
+    v_, s_, t_ = g.vector, g.scalar, g.tensor
+    A, F = AluOpType, ActivationFunctionType
+    cnt = {"v": 0, "s": 0, "t": 0}
+    seen = {}
+    queues = {"g": g, "v": v_, "s": s_, "t": t_, "y": g.sync}
+
+    def done(ins, q):
+        ins.then_inc(T.sem[q], 1)
+        cnt[q] += 1
+        return cnt[q]
+
+    def wait(q, sem, val):
+        if val > seen.get((q, sem), 0):
+            seen[q, sem] = val
+            queues[q].wait_ge(T.sem[sem], val)
+
+    def load_list(q, buf, src, sem, ks):
+        for k in ks:
+            q.dma_start(T[buf][16 * k:16 * k + 16, :], T[src][:, :]).then_inc(T.sem[sem], 16)
+
+    s_.dma_start(T.xs[:, :], T.x[:, :]).then_inc(T.sem.dx, 16)
+    load_list(g.sync, "lsa", "snd1", "dsa", range(0, 5))
+    load_list(s_, "lsa", "snd1", "dsa", range(5, 8))
+    g.sync.dma_start(T.w1s[:, :], T.w1[:, :]).then_inc(T.sem.dw1, 16)
+    g.sync.dma_start(T.lrb[:, :], T.src2[:, :]).then_inc(T.sem.drb, 16)
+    load_list(g.sync, "lra", "src1", "dra", range(8))
+    g.sync.dma_start(T.w2s[:, :], T.w2[:, :]).then_inc(T.sem.dw2, 16)
+    load_list(g.sync, "lsb", "snd2", "dsb", range(8))
+
+    for t in range(4):
+        done(v_.memset(T.mk[:, t:4 * NODES:4], 1.0 if t else 0.0), "v")
+    for i in range(4):
+        done(v_.memset(T["tb%d" % i][:, NODES + rank * C1:NODES + (rank + 1) * C1], 0.0), "v")
+    const = done(v_.memset(T.ut[:, NODES + rank * C2:NODES + (rank + 1) * C2], 0.0), "v")
+
+    wait("v", "dsa", 128)
+    osa = {}
+    for t in (2, 3, 0, 1):
+        osa[t] = done(v_.tensor_scalar(T.osa[:, S1W * t:S1W * (t + 1)], T.lsa[:, :], 4, t, A.mult, A.add), "v")
+
+    def pick(q, out, layer, t, c0, c1):
+        o = T[out][:, 4 * c0 + t:4 * c1:4]
+        k0, k1 = c0 // 16, c1 // 16
+        if layer == 1:
+            i = T.xs[:, 0:4 * NODES].indirect(T.osa[:, S1W * t + k0:S1W * t + k1])
+        elif t < 2:
+            i = T["r%d" % t][:, 0:NODES].indirect(T.osb[:, k0:k1])
+        else:
+            i = T["sc%d" % t][:, 0:4 * NODES].indirect(T.osc[:, k0:k1])
+        return done(v_.tensor_copy(o, i), "v") if q == "v" else done(s_.activation(o, i, F.Copy), "s")
+
+    def quantise(out, runs, codes, planes):
+        for a, b in runs:
+            qd = done(v_.quantize_mx(T[codes][:, a:b], T[planes][:, a:b], T[out][:, 4 * a:4 * b]), "v")
+        return qd
+
+    est = {"v": 0.0, "s": 0.0}
+
+    def gather(a, b):
+        n = b - a
+        k = (4 * n + (est["v"] - est["s"]) / 1.6) / 2
+        k = min(4 * n, max(0, int(round(k / 32)) * 32))
+        last = {"s": 0, "v": 0}
+        for j, t in enumerate((2, 3, 0, 1)):
+            m = a + min(n, max(0, k - j * n))
+            for q, c0, c1 in (("s", a, m), ("v", m, b)):
+                if c1 > c0:
+                    est[q] += 60 + 1.6 * (c1 - c0)
+                    wait(q, "v", osa[t])
+                    last[q] = pick(q, "xg", 1, t, c0, c1)
+        wait("v", "v", last["v"])
+        wait("v", "s", last["s"])
+        est["v"] = max(est.values()) + 12 + 1.1 * n
+        return quantise("xg", [(a, b)], "xsc", "xss")
+
+    def send(items, sc, ss):
+        for m in (0, 1):
+            tr = []
+            for c, bufs, d0, sems, c0, n, eng in items:
+                d, s = T[bufs[m]][:, d0:d0 + n], T[(sc, ss)[m]][:, c0:c0 + n]
+                if m == 0:
+                    d, s = u8(d), u8(s)
+                rid, pid, _ = topo.addr(c)
+                tr.append(RemoteDMATransfer(dst_ids=[DstId(rid=rid, pnc=pid)], dma_engine_mask=bits(eng),
+                                            remote_sem=T.sem[sems[m]], src=s, dst=d))
+            g.remote_dma_fused(tr, local_sem=T.sem.loc)
+        return 2 * sum(len(x[6]) for x in items)
+
+    def takes(road):
+        b = goes[road]
+        mid = roads[me, b][1]
+        ks = [k for k in firsts(mine, len(ranks[b])) if ranks[b][k] != rank]
+        return [(k, ranks[b][k], mid[mine] if mid else T.cores[ranks[b][k]]) for k in ks]
+
+    def unit(road, h):
+        k, r, c = takes(road)[h]
+        eng = send_engines(core, c, T, topo)
+        if road in (MATE, DIE):
+            return (c, ("f1c", "f1s"), k * C1, ("fc1" + "ab"[h], "fs1" + "ab"[h]), r * C1, C1, eng)
+        return (c, ("xrc", "xrs"), rank * C1, ("x%d" % rank,) * 2, r * C1, C1, eng)
+
+    def writer(road, k):
+        a = came[road]
+        mid = roads[a, me][1]
+        c = mid[k] if mid else T.cores[ranks[a][k]]
+        return len(send_engines(c, core, T, topo)) if T.rank_of(c) is not None else len(topo.engines(c, core))
+
+    free = {}
+    taken = {"v": 0, "s": 0}
+    half = [0]
+
+    def multiply(road, h, own):
+        if road is None:
+            cb, pb, c0, w, o0 = "xoc", "xos", 0, NODES, 0
+            wait("t", "v", own)
+        else:
+            ks = [k for k in firsts(mine, len(ranks[came[road]])) if ranks[came[road]][k] != rank]
+            r = ranks[came[road]][ks[h]]
+            cb, pb, c0, w, o0 = "xrc", "xrs", r * C1, C1, NODES + r * C1
+            wait("t", "x%d" % r, 2 * writer(road, ks[h]))
+        banks = [512 * (half[0] + i) for i in range(4)]
+        half[0] = 4 - half[0]
+        mm = []
+        for i, bank in enumerate(banks):
+            if bank in free:
+                wait("t", *free[bank])
+            mm.append(done(t_.matmul_mx(T.pp[:, bank:bank + w], T.w1c[:, 128 * i:128 * i + 128], T.w1p[:, 128 * i:128 * i + 128],
+                                        T[cb][:, c0:c0 + w], T[pb][:, c0:c0 + w], True, True), "t"))
+        for i, bank in enumerate(banks):
+            q = "s" if est["s"] <= est["v"] else "v"
+            est[q] += 50 + 1.05 * w
+            wait(q, "t", mm[i])
+            out, z = T["tb%d" % i][:, o0:o0 + w], T.pp[:, bank:bank + w]
+            if q == "v":
+                taken[q] = done(v_.tensor_scalar(out, z, 0.0, 0.05, A.max, A.mult), "v")
+            else:
+                taken[q] = done(s_.activation(out, z, F.Relu, scale=0.05), "s")
+            free[bank] = (q, taken[q])
+
+    sent = 0
+    own = lists = 0
+    held = []
+    wait("v", "dx", 16)
+    wait("s", "dx", 16)
+    for what, road, h in PLAN:
+        if what in ("send", "hold"):
+            item = unit(road, h)
+            held.append(item)
+            qd = gather(item[4], item[4] + item[5])
+            if what == "send":
+                wait("g", "v", qd)
+                sent += send(held, "xsc", "xss")
+                held = []
+        elif what == "take":
+            multiply(road, h, own)
+        elif what == "self":
+            wait("v", "dw1", 16)
+            done(v_.quantize_mx(T.w1c[:, :], T.w1p[:, :], T.w1s[:, :]), "v")
+            own = done(v_.quantize_mx(T.xoc[:, :], T.xos[:, :], T.xs[:, :]), "v")
+            est["v"] += 1150
+        elif what == "rows":
+            wait("v", "dra", 128)
+            wait("v", "drb", 16)
+            for b in range(4):
+                done(v_.tensor_copy(T.ecol[0:16, EW * b:EW * b + E1], T.lra[0:16, b:R1W:4]), "v")
+                ec = done(v_.tensor_copy(T.ecol[0:16, EW * b + E1:EW * (b + 1)], T.lrb[0:16, b:R2W:4]), "v")
+            est["v"] += 560
+            wait("y", "v", ec)
+            for e in range(4):
+                for b in range(4):
+                    g.sync.dma_start(T.erow[4 * b:4 * b + 4, EW * e:EW * (e + 1)],
+                                     T.ecol[e:16:4, EW * b:EW * (b + 1)]).then_inc(T.sem.der, 16)
+            g.sync.wait_ge(T.sem.der, 256)
+            load_list(g.sync, "ore", "erow", "dre", range(8))
+        else:
+            wait("v", "dw2", 16)
+            done(v_.quantize_mx(T.w2c[:, :], T.w2p[:, :], T.w2s[:, :]), "v")
+            done(v_.tensor_copy(T.ora[:, :], T.lra[:, :]), "v")
+            wait("v", "dsb", 128)
+            done(v_.tensor_copy(T.osb[:, :], T.lsb[:, :]), "v")
+            lists = done(v_.tensor_scalar(T.osc[:, :], T.lsb[:, :], 4, 3, A.mult, A.add), "v")
+            est["v"] += 450
+
+    for q in "vs":
+        wait(q, "dre", 128)
+        wait(q, "v", max(taken["v"], lists, const))
+        wait(q, "s", taken["s"])
+    first = [(T["gg%d" % i][:, 0:NODES], T["tb%d" % i][:, 0:W].indirect(T.ore[:, 0:E1])) for i in (0, 1)]
+    acc = {0: ("s", done(s_.activation(*first[0], F.Copy), "s")), 1: ("v", done(v_.tensor_copy(*first[1]), "v"))}
+    pieces = {2: [(0, R1W)], 3: [(0, R1W // 2), (R1W // 2, 3 * R1W // 4), (3 * R1W // 4, R1W)]}
+    gs = {}
+    for i in (2, 3):
+        for a, b in pieces[i]:
+            gs[i, a] = done(s_.activation(T["gg%d" % i][:, 16 * a:16 * b], T["tb%d" % i][:, 0:W].indirect(T.ora[:, a:b]), F.Copy), "s")
+    for e in (1, 2, 3):
+        for i in (0, 1):
+            wait("v", *acc[i])
+            out = T["gg%d" % i][:, NODES * e:NODES * (e + 1)] if e < 3 else T["r%d" % i][:, :]
+            acc[i] = ("v", done(v_.tensor_tensor(out, T["tb%d" % i][:, 0:W].indirect(T.ore[:, EW * e:EW * e + E1]),
+                                                 T["gg%d" % i][:, NODES * (e - 1):NODES * e], A.max), "v"))
+    rd = {0: acc[0][1], 1: acc[1][1]}
+    for i in (2, 3):
+        for a, b in pieces[i]:
+            wait("v", "s", gs[i, a])
+            a, b = 16 * a, 16 * b
+            rd[i] = done(v_.tensor_tensor_scan(T["sc%d" % i][:, a:b], T.mk[:, a:b], T["gg%d" % i][:, a:b], 0.0, A.mult, A.max), "v")
+
+    for pair, whose in (((MATE, DIE), ("ss", "ss", "sv", "vv")), ((DIRECT, OWN), ("ss", "ss", "vv", "vv"))):
+        items = []
+        for road in pair:
+            to = takes(road)
+            eng = send_engines(core, to[0][2], T, topo)
+            if road in (MATE, DIE):
+                items.append((to[0][2], ("f2c", "f2s"), 0, ("fc2", "fs2"), ranks[goes[road]][0] * C2, len(to) * C2, eng))
+                continue
+            e = len(eng) // len(to)
+            for n, (k, r, c) in enumerate(to):
+                bufs, at = (("hrc", "hrs"), rank * C2) if road == DIRECT else (("hoc", "hos"), NODES)
+                items.append((c, bufs, at, ("h%d" % rank,) * 2, r * C2, C2, eng[e * n:e * n + e]))
+        cols = [(ranks[goes[road]][0] * C2, (ranks[goes[road]][-1] + 1) * C2) for road in pair]
+        last = {}
+        for t in range(4):
+            for q in "sv":
+                for a, b in join([c for c, w in zip(cols, whose[t]) if w == q]):
+                    wait(q, "v", max(rd[t], lists))
+                    last[q] = pick(q, "hg", 2, t, a, b)
+        wait("v", "v", last["v"])
+        wait("v", "s", last["s"])
+        qd = quantise("hg", join(cols), "hsc", "hss")
+        wait("g", "v", qd)
+        sent += send(items, "hsc", "hss")
+    for i in (0, 1):
+        hs = done(s_.activation(T.ht[:, i:4 * NODES:4], T["r%d" % i][:, :], F.Copy), "s")
+    for i in (2, 3):
+        hv = done(v_.tensor_copy(T.ht[:, i:4 * NODES:4], T["sc%d" % i][:, 3:4 * NODES:4]), "v")
+    wait("v", "v", hv)
+    wait("v", "s", hs)
+    qh = done(v_.quantize_mx(T.hoc[:, 0:NODES], T.hos[:, 0:NODES], T.ht[:, :]), "v")
+
+    blocks = [("hoc", "hos", 0, NODES, 0, 0, []),
+              ("hoc", "hos", NODES + C2 - 128, 128, 128 - C2, NODES + near[0] * C2, [("h%d" % near[0], 2 * writer(OWN, 1 - mine))])]
+    for road in (DIRECT, DIE, MATE):
+        rs = ranks[came[road]]
+        sems = [("h%d" % r, 2 * writer(road, k) // len(ranks[me])) for k, r in enumerate(rs)]
+        blocks.append(("hrc", "hrs", rs[0] * C2, len(rs) * C2, 0, NODES + rs[0] * C2, sems))
+    wait("t", "v", qh)
+    wait("t", "s", taken["s"])
+    uq = {"v": 0, "s": 0}
+    for n, (cb, pb, c0, w, skip, o0, sems) in enumerate(blocks):
+        for sem, val in sems:
+            wait("t", sem, val)
+        m = done(t_.matmul_mx(T.pp[:, 512 * n:512 * n + w], T.w2c[:, :], T.w2p[:, :], T[cb][:, c0:c0 + w], T[pb][:, c0:c0 + w],
+                              True, True), "t")
+        out, z = T.ut[:, o0:o0 + w - skip], T.pp[:, 512 * n + skip:512 * n + w]
+        q = "sv"[n % 2]
+        wait(q, "t", m)
+        uq[q] = done(s_.activation(out, z, F.Copy), "s") if q == "s" else done(v_.tensor_copy(out, z), "v")
+
+    for q in "sv":
+        wait(q, "v", uq["v"])
+        wait(q, "s", uq["s"])
+
+    def source(e, k):
+        return T.ut[:, 0:U].indirect(T.ore[:, EW * e + E1 + E2 // 2 * k:EW * e + E1 + E2 // 2 * (k + 1)])
+
+    hw = TARGETS // 2
+    up = [("s", done(s_.activation(T.g2[:, hw * k:hw * (k + 1)], source(0, k), F.Copy), "s")) for k in (0, 1)]
+    for e in (1, 2, 3):
+        for k in (0, 1):
+            wait("v", *up[k])
+            out = T.g2[:, TARGETS * e + hw * k:TARGETS * e + hw * (k + 1)] if e < 3 else T.yo[:, hw * k:hw * (k + 1)]
+            up[k] = ("v", done(v_.tensor_tensor(out, source(e, k), T.g2[:, TARGETS * (e - 1) + hw * k:TARGETS * (e - 1) + hw * (k + 1)],
+                                                A.max), "v"))
+    for k in (0, 1):
+        wait("y", *up[k])
+        g.sync.dma_start(T.y[:, hw * k:hw * (k + 1)], T.yo[:, hw * k:hw * (k + 1)]).then_inc(T.sem.dy, 16)
+    for q in "vst":
+        wait("y", q, cnt[q])
+    g.sync.wait_ge(T.sem.dy, 32)
+    g.wait_ge(T.sem.loc, sent)

@@ -10,6 +10,8 @@ S1W, S2W = N * C1 // 16, N * C2 // 16
 R1W, R2W = 4 * NODES // 16, 4 * TARGETS // 16
 E1, E2 = NODES // 16, TARGETS // 16
 EW = E1 + E2
+ORA, OSB, OSC, OW = 4 * EW, 4 * EW + R1W, 4 * EW + R1W + S2W, 4 * EW + R1W + 2 * S2W
+BANK, BANKS = 512, 8
 MXC, MXS = "float8_e4m3fn_x4", "uint8"
 
 SCRATCH = {
@@ -17,29 +19,21 @@ SCRATCH = {
     "w1s": ("sbuf", [128, 4 * 512], "bfloat16"),
     "w2s": ("sbuf", [128, 4 * 128], "bfloat16"),
     "lsa": ("sbuf", [128, S1W], "int32"),
-    "lsb": ("sbuf", [128, S2W], "int32"),
-    "lra": ("sbuf", [128, R1W], "int32"),
-    "lrb": ("sbuf", [16, R2W], "int32"),
     "osa": ("sbuf", [128, 4 * S1W], "uint16"),
-    "osb": ("sbuf", [128, S2W], "uint16"),
-    "osc": ("sbuf", [128, S2W], "uint16"),
-    "ora": ("sbuf", [128, R1W], "uint16"),
-    "ecol": ("sbuf", [128, 4 * EW], "uint16"),
-    "erow": ("dram", [16, 4 * EW], "uint16"),
-    "ore": ("sbuf", [128, 4 * EW], "uint16"),
+    "lr": ("sbuf", [16, 5, 4 * EW + 4], "int32"),
+    "ore": ("sbuf", [128, OW], "uint16"),
     "xg": ("sbuf", [128, 4 * N * C1], "bfloat16"),
     "xsc": ("sbuf", [128, N * C1], MXC), "xss": ("sbuf", [128, N * C1], MXS),
-    "xoc": ("sbuf", [128, NODES], MXC), "xos": ("sbuf", [128, NODES], MXS),
-    "xrc": ("sbuf", [128, N * C1], MXC), "xrs": ("sbuf", [128, N * C1], MXS),
+    "xc": ("sbuf", [128, W], MXC), "xp": ("sbuf", [128, W], MXS),
     "w1c": ("sbuf", [128, 512], MXC), "w1p": ("sbuf", [128, 512], MXS),
     "w2c": ("sbuf", [128, 128], MXC), "w2p": ("sbuf", [128, 128], MXS),
     "tb0": ("sbuf", [128, W], "bfloat16"), "tb1": ("sbuf", [128, W], "bfloat16"),
     "tb2": ("sbuf", [128, W], "bfloat16"), "tb3": ("sbuf", [128, W], "bfloat16"),
-    "gg0": ("sbuf", [128, 3 * NODES], "bfloat16"), "gg1": ("sbuf", [128, 3 * NODES], "bfloat16"),
+    "gg0": ("sbuf", [128, 4 * NODES], "bfloat16"), "gg1": ("sbuf", [128, 4 * NODES], "bfloat16"),
     "gg2": ("sbuf", [128, 4 * NODES], "bfloat16"), "gg3": ("sbuf", [128, 4 * NODES], "bfloat16"),
-    "sc2": ("sbuf", [128, 4 * NODES], "bfloat16"), "sc3": ("sbuf", [128, 4 * NODES], "bfloat16"),
-    "mk": ("sbuf", [128, 4 * NODES], "bfloat16"),
-    "r0": ("sbuf", [128, NODES], "bfloat16"), "r1": ("sbuf", [128, NODES], "bfloat16"),
+    "r0": ("sbuf", [128, 4 * NODES], "bfloat16"), "r1": ("sbuf", [128, 4 * NODES], "bfloat16"),
+    "r2": ("sbuf", [128, 4 * NODES], "bfloat16"), "r3": ("sbuf", [128, 4 * NODES], "bfloat16"),
+    "mk": ("sbuf", [128, 2 * NODES], "bfloat16"),
     "ht": ("sbuf", [128, 4 * NODES], "bfloat16"),
     "hg": ("sbuf", [128, 4 * N * C2], "bfloat16"),
     "hsc": ("sbuf", [128, N * C2], MXC), "hss": ("sbuf", [128, N * C2], MXS),
@@ -50,17 +44,33 @@ SCRATCH = {
     "yo": ("sbuf", [128, TARGETS], "float32"),
     "f1c": ("sbuf", [128, 2 * C1], MXC), "f1s": ("sbuf", [128, 2 * C1], MXS),
     "f2c": ("sbuf", [128, 2 * C2], MXC), "f2s": ("sbuf", [128, 2 * C2], MXS),
-    "pp": ("psum", [128, 512 * 8], "float32"),
+    "pp": ("psum", [128, BANK * BANKS], "float32"),
 }
-SEMAPHORES = (["v", "s", "t", "loc", "dx", "dw1", "dw2", "dsa", "dsb", "dra", "drb", "der", "dre", "dy"]
-              + ["fc1a", "fs1a", "fc1b", "fs1b", "fc2", "fs2"]
+SEMAPHORES = (["v", "s", "t", "loc", "dx", "dw1", "dw2", "dsa", "dr", "dre", "dy", "f100", "f101", "f110", "f111", "f2"]
               + ["x%d" % r for r in range(N)] + ["h%d" % r for r in range(N)])
 
 MATE, DIE, DIRECT, OWN = "mate", "die", "direct", "own"
 
-PLAN = (("send", MATE, 0), ("self", None, 0), ("send", DIE, 0), ("hold", OWN, 0), ("send", MATE, 1), ("send", DIE, 1),
-        ("send", DIRECT, 0), ("rows", None, 0), ("take", None, 0), ("send", DIRECT, 1), ("take", OWN, 0), ("lists", None, 0),
-        ("take", MATE, 0), ("take", DIE, 0), ("take", DIRECT, 0), ("take", MATE, 1), ("take", DIE, 1), ("take", DIRECT, 1))
+M0, M1, D0, D1, R0, R1, O0 = (MATE, 0), (MATE, 1), (DIE, 0), (DIE, 1), (DIRECT, 0), (DIRECT, 1), (OWN, 0)
+SENDS = [(([M0], []), ([D0], [M0, D0]), ([R0], [R0]), ([M1], []), ([D1], [M1, D1]), ([R1], []), ([O0], [R1, O0])),
+         (([D0], []), ([M0], [M0, D0]), ([R0], [R0]), ([D1], []), ([M1], [M1, D1]), ([R1], []), ([O0], [R1, O0]))]
+NOLAG = (0, 6)
+SOLO = 0
+AHEAD, BEHIND, LISTS, LAG, SORT = 4, 0, 6, 0, 420
+NEARBY = False
+ARRIVE = [(R0, M0, D0, O0, D1, R1, M1), (R0, D0, M0, O0, M1, R1, D1)]
+WEIGHTS, MINE, TAKE = 2, 3, (6,)
+LATE = (0, 0, 0, 0)
+FOLDED, LEAD, SNAP, EMPTIES, WHOLE = (0, 1), "vs", 96, "svsvsv", "ssvv"
+PICKS = (((1, "s", MATE), (1, "v", DIE)),
+         ((3, "s", DIRECT, OWN), (2, "s", DIRECT, OWN), (0, "v", DIRECT, OWN), (1, "v", DIRECT, OWN)))
+LAST = {2: "s", 0: "v", 3: "s", 1: "v"}
+MAXIMA = (("all", 2, "s", 0, 256), ("first", 0, "v", 0, 512), ("all", 2, "s", 256, 512), ("fold", 0, 1), ("scan", 2, 0, 256),
+          ("first", 1, "s", 0, 384), ("first", 1, "v", 384, 512),
+          ("fold", 0, 2), ("scan", 2, 256, 512), ("fold", 1, 1), ("fold", 0, 3),
+          ("all", 3, "s", 0, 256), ("all", 3, "s", 256, 512), ("pick", 2, "s", MATE, DIE), ("pick", 0, "s", MATE, DIE),
+          ("scan", 3, 0, 256), ("fold", 1, 2), ("scan", 3, 256, 512), ("fold", 1, 3), ("pick", 3, "s", MATE, DIE))
+CALL, GATHER, EMPTY, PACK = 55, 1.4, 0.87, 0.23
 
 
 def layout(T, topo):
@@ -80,15 +90,16 @@ def layout(T, topo):
             src, dst = T.cores[ranks[a][0]], T.cores[ranks[b][0]]
             k = len(ranks[a])
             if topo.same_plane(a, b):
-                mid = [c for c in topo.cores_of(src) if topo.die(c) != topo.die(src) and topo.may_write(c, dst)
-                       and T.rank_of(c) is None]
-                roads[a, b] = (DIE, mid[:k])
+                mid = [c for c in topo.cores_of(src) if topo.may_write(c, dst) and T.rank_of(c) is None]
+                far = [c for c in mid if topo.die(c) != topo.die(src)]
+                roads[a, b] = (DIE, far[:k] + ([c for c in mid if c not in far][:k] if NEARBY else far[k:2 * k]))
             elif (ib - ia) % len(chips) == 1:
                 roads[a, b] = (DIRECT, None)
             else:
-                mid = [c for c in range(SIM_CORES) if topo.mates(topo.chip(c), b) and topo.die(c) == topo.die(dst)
+                mid = [c for c in range(SIM_CORES) if topo.mates(topo.chip(c), b)
                        and topo.may_write(c, dst) and topo.may_write(src, c) and T.rank_of(c) is None]
-                roads[a, b] = (MATE, mid[:k])
+                dies = [[c for c in mid if (topo.die(c) != topo.die(dst)) == far] for far in (False, True)]
+                roads[a, b] = (MATE, [dies[(j + m) % 2][j] for m in range(2) for j in range(k)])
     return chips, ranks, roads
 
 
@@ -116,41 +127,42 @@ def send_engines(src, dst, T, topo):
     return [k for k in e if k not in off]
 
 
+def beside(call, u):
+    return [x for x in call if (x[0] in (MATE, DIRECT)) == (u[0] in (MATE, DIRECT))]
+
+
 def hand_on(g, core, T, topo):
     chips, ranks, roads = layout(T, topo)
     for (a, b), (road, mid) in roads.items():
         if not mid or core not in mid:
             continue
-        k = mid.index(core)
+        m, k = divmod(mid.index(core), len(ranks[a]))
+        view = (u8, lambda v: v)[m]
         s = ranks[a][k]
         n = len(ranks[b])
         w = len(send_engines(T.cores[s], core, T, topo))
         sent = 0
-        for h, d in enumerate(firsts(k, n)):
+        for (h, c0, c1), j in [((u + (0, C1))[1:4], len(beside(step[m], u))) for step in SENDS[k] for u in step[m] if u[0] == road]:
+            d = firsts(k, n)[h]
             dst = T.cores[ranks[b][d]]
             rid, pid, _ = topo.addr(dst)
             eng = topo.engines(core, dst)
-            arr = T.sem["x%d" % s]
-            g.wait_ge(T.sem["fc1" + "ab"[h]], w)
-            g.remote_dma(u8(T.xrc[:, s * C1:(s + 1) * C1]), u8(T.f1c[:, d * C1:(d + 1) * C1]), arr, T.sem.loc, pid, rid, bits(eng))
-            g.wait_ge(T.sem["fs1" + "ab"[h]], w)
-            g.remote_dma(T.xrs[:, s * C1:(s + 1) * C1], T.f1s[:, d * C1:(d + 1) * C1], arr, T.sem.loc, pid, rid, bits(eng))
-            sent += 2 * len(eng)
-        for sem, out, buf in (("fc2", "hrc", "f2c"), ("fs2", "hrs", "f2s")):
-            tr = []
-            for d in range(n):
-                dst = T.cores[ranks[b][d]]
-                rid, pid, _ = topo.addr(dst)
-                eng = topo.engines(core, dst)
-                e = len(eng) // n
-                o, i = T[out][:, s * C2:(s + 1) * C2], T[buf][:, d * C2:(d + 1) * C2]
-                if out == "hrc":
-                    o, i = u8(o), u8(i)
-                tr.append(RemoteDMATransfer(dst_ids=[DstId(rid=rid, pnc=pid)], dma_engine_mask=bits(eng[e * d:e * d + e]),
-                                            remote_sem=T.sem["h%d" % s], src=i, dst=o))
-                sent += e
-            g.wait_ge(T.sem[sem], w)
-            g.remote_dma_fused(tr, local_sem=T.sem.loc)
+            o, i = T[("xc", "xp")[m]][:, NODES + s * C1 + c0:NODES + s * C1 + c1], T[("f1c", "f1s")[m]][:, d * C1 + c0:d * C1 + c1]
+            g.wait_ge(T.sem["f1%d%d" % (h, c1 < C1)], w // j)
+            g.remote_dma(view(o), view(i), T.sem["x%d" % s], T.sem.loc, pid, rid, bits(eng))
+            sent += len(eng)
+        tr = []
+        for d in range(n):
+            dst = T.cores[ranks[b][d]]
+            rid, pid, _ = topo.addr(dst)
+            eng = topo.engines(core, dst)
+            e = len(eng) // n
+            o, i = T[("hrc", "hrs")[m]][:, s * C2:(s + 1) * C2], T[("f2c", "f2s")[m]][:, d * C2:(d + 1) * C2]
+            tr.append(RemoteDMATransfer(dst_ids=[DstId(rid=rid, pnc=pid)], dma_engine_mask=bits(eng[e * d:e * d + e]),
+                                        remote_sem=T.sem["h%d" % s], src=view(i), dst=view(o)))
+            sent += e
+        g.wait_ge(T.sem.f2, w)
+        g.remote_dma_fused(tr, local_sem=T.sem.loc)
         g.wait_ge(T.sem.loc, sent)
 
 
@@ -191,23 +203,32 @@ def rank_program(g, core, T, topo):
             seen[q, sem] = val
             queues[q].wait_ge(T.sem[sem], val)
 
+    def after(q, marks):
+        for sem, val in marks.items():
+            wait(q, sem, val)
+
     def load_list(q, buf, src, sem, ks):
         for k in ks:
             q.dma_start(T[buf][16 * k:16 * k + 16, :], T[src][:, :]).then_inc(T.sem[sem], 16)
 
+    load_list(s_, "lsa", "snd1", "dsa", range(0, AHEAD))
     s_.dma_start(T.xs[:, :], T.x[:, :]).then_inc(T.sem.dx, 16)
-    load_list(g.sync, "lsa", "snd1", "dsa", range(0, 5))
-    load_list(s_, "lsa", "snd1", "dsa", range(5, 8))
+    load_list(s_, "lsa", "snd1", "dsa", range(AHEAD, AHEAD + BEHIND))
+    load_list(g.sync, "lsa", "snd1", "dsa", range(AHEAD + BEHIND, 8))
+    wait("y", "dsa", 128)
     g.sync.dma_start(T.w1s[:, :], T.w1[:, :]).then_inc(T.sem.dw1, 16)
-    g.sync.dma_start(T.lrb[:, :], T.src2[:, :]).then_inc(T.sem.drb, 16)
-    load_list(g.sync, "lra", "src1", "dra", range(8))
     g.sync.dma_start(T.w2s[:, :], T.w2[:, :]).then_inc(T.sem.dw2, 16)
-    load_list(g.sync, "lsb", "snd2", "dsb", range(8))
+    for b in range(4):
+        g.sync.dma_start(T.lr[4 * b:4 * b + 4, 0:4, 4 - b:4 - b + R1W], T.src1[:, :]).then_inc(T.sem.dr, 16)
+        g.sync.dma_start(T.lr[4 * b:4 * b + 4, 0:4, 4 - b + R1W:4 - b + 4 * EW], T.src2[:, :]).then_inc(T.sem.dr, 16)
+    g.sync.dma_start(T.lr[:, 4, 0:R1W], T.src1[:, :]).then_inc(T.sem.dr, 16)
+    g.sync.dma_start(T.lr[:, 4, R1W:R1W + S2W], T.snd2[:, :]).then_inc(T.sem.dr, 16)
 
     for t in range(4):
-        done(v_.memset(T.mk[:, t:4 * NODES:4], 1.0 if t else 0.0), "v")
+        done(v_.memset(T.mk[:, t:2 * NODES:4], 1.0 if t else 0.0), "v")
     for i in range(4):
         done(v_.memset(T["tb%d" % i][:, NODES + rank * C1:NODES + (rank + 1) * C1], 0.0), "v")
+    done(v_.memset(T.hg[:, 4 * rank * C2:4 * (rank + 1) * C2], 0.0), "v")
     const = done(v_.memset(T.ut[:, NODES + rank * C2:NODES + (rank + 1) * C2], 0.0), "v")
 
     wait("v", "dsa", 128)
@@ -215,66 +236,47 @@ def rank_program(g, core, T, topo):
     for t in (2, 3, 0, 1):
         osa[t] = done(v_.tensor_scalar(T.osa[:, S1W * t:S1W * (t + 1)], T.lsa[:, :], 4, t, A.mult, A.add), "v")
 
-    def pick(q, out, layer, t, c0, c1):
-        o = T[out][:, 4 * c0 + t:4 * c1:4]
-        k0, k1 = c0 // 16, c1 // 16
-        if layer == 1:
-            i = T.xs[:, 0:4 * NODES].indirect(T.osa[:, S1W * t + k0:S1W * t + k1])
-        elif t < 2:
-            i = T["r%d" % t][:, 0:NODES].indirect(T.osb[:, k0:k1])
-        else:
-            i = T["sc%d" % t][:, 0:4 * NODES].indirect(T.osc[:, k0:k1])
-        return done(v_.tensor_copy(o, i), "v") if q == "v" else done(s_.activation(o, i, F.Copy), "s")
+    def other_lists():
+        wait("v", "dr", 10 * 16)
+        done(v_.tensor_copy(T.ore[0:16, 0:ORA], T.lr[:, 0:4, 4:4 + 4 * EW:4]), "v")
+        done(v_.tensor_copy(T.ore[0:16, ORA:OSC], T.lr[:, 4, 0:R1W + S2W]), "v")
+        wait("y", "v", done(v_.tensor_scalar(T.ore[0:16, OSC:OW], T.lr[:, 4, R1W:R1W + S2W], 4, 3, A.mult, A.add), "v"))
+        for k in range(1, 8):
+            g.sync.dma_start(T.ore[16 * k:16 * k + 16, :], T.ore[0:16, :]).then_inc(T.sem.dre, 16)
 
-    def quantise(out, runs, codes, planes):
-        for a, b in runs:
-            qd = done(v_.quantize_mx(T[codes][:, a:b], T[planes][:, a:b], T[out][:, 4 * a:4 * b]), "v")
-        return qd
+    lists = {"dre": 7 * 16}
 
-    est = {"v": 0.0, "s": 0.0}
+    def copy(q, out, in_):
+        return done(v_.tensor_copy(out, in_), "v") if q == "v" else done(s_.activation(out, in_, F.Copy), "s")
 
-    def gather(a, b):
-        n = b - a
-        k = (4 * n + (est["v"] - est["s"]) / 1.6) / 2
-        k = min(4 * n, max(0, int(round(k / 32)) * 32))
-        last = {"s": 0, "v": 0}
-        for j, t in enumerate((2, 3, 0, 1)):
-            m = a + min(n, max(0, k - j * n))
-            for q, c0, c1 in (("s", a, m), ("v", m, b)):
-                if c1 > c0:
-                    est[q] += 60 + 1.6 * (c1 - c0)
-                    wait(q, "v", osa[t])
-                    last[q] = pick(q, "xg", 1, t, c0, c1)
-        wait("v", "v", last["v"])
-        wait("v", "s", last["s"])
-        est["v"] = max(est.values()) + 12 + 1.1 * n
-        return quantise("xg", [(a, b)], "xsc", "xss")
-
-    def send(items, sc, ss):
-        for m in (0, 1):
+    def send(items, sc, ss, parts=(0, 1)):
+        for m in parts:
             tr = []
-            for c, bufs, d0, sems, c0, n, eng in items:
+            for cs, bufs, d0, sem, c0, n, eng in items:
                 d, s = T[bufs[m]][:, d0:d0 + n], T[(sc, ss)[m]][:, c0:c0 + n]
                 if m == 0:
                     d, s = u8(d), u8(s)
-                rid, pid, _ = topo.addr(c)
+                rid, pid, _ = topo.addr(cs[m])
                 tr.append(RemoteDMATransfer(dst_ids=[DstId(rid=rid, pnc=pid)], dma_engine_mask=bits(eng),
-                                            remote_sem=T.sem[sems[m]], src=s, dst=d))
+                                            remote_sem=T.sem[sem], src=s, dst=d))
             g.remote_dma_fused(tr, local_sem=T.sem.loc)
-        return 2 * sum(len(x[6]) for x in items)
+        return len(parts) * sum(len(x[6]) for x in items)
 
     def takes(road):
         b = goes[road]
         mid = roads[me, b][1]
         ks = [k for k in firsts(mine, len(ranks[b])) if ranks[b][k] != rank]
-        return [(k, ranks[b][k], mid[mine] if mid else T.cores[ranks[b][k]]) for k in ks]
+        return [(k, ranks[b][k], mid[mine::len(ranks[me])] if mid else [T.cores[ranks[b][k]]] * 2) for k in ks]
 
-    def unit(road, h):
-        k, r, c = takes(road)[h]
-        eng = send_engines(core, c, T, topo)
+    def unit(call, u):
+        road, h, a, b = (u + (0, C1))[:4]
+        k, r, cs = takes(road)[h]
+        eng, with_u = send_engines(core, cs[0], T, topo), beside(call, u)
+        e = len(eng) // len(with_u)
+        eng = eng[e * with_u.index(u):e * with_u.index(u) + e]
         if road in (MATE, DIE):
-            return (c, ("f1c", "f1s"), k * C1, ("fc1" + "ab"[h], "fs1" + "ab"[h]), r * C1, C1, eng)
-        return (c, ("xrc", "xrs"), rank * C1, ("x%d" % rank,) * 2, r * C1, C1, eng)
+            return (cs, ("f1c", "f1s"), k * C1 + a, "f1%d%d" % (h, b < C1), r * C1 + a, b - a, eng)
+        return (cs, ("xc", "xp"), NODES + rank * C1 + a, "x%d" % rank, r * C1 + a, b - a, eng)
 
     def writer(road, k):
         a = came[road]
@@ -282,171 +284,220 @@ def rank_program(g, core, T, topo):
         c = mid[k] if mid else T.cores[ranks[a][k]]
         return len(send_engines(c, core, T, topo)) if T.rank_of(c) is not None else len(topo.engines(c, core))
 
+    est = {"v": LAG, "s": 0.0}
+
+    def pieces(runs, owed):
+        n, parts = runs[0][1] - runs[0][0], [(t, a, b) for t in (2, 3, 0, 1) for a, b in runs]
+        k = min(n * len(parts), max(0, 32 * round((n * len(parts) + (est["v"] + owed - est["s"]) / GATHER) / 64)))
+        k = min((k, n * round(k / n)), key=lambda m: abs(m - k) - (SNAP if m % n == 0 else 0))
+        cut = [(t, a, a + min(n, max(0, k - j * n)), b) for j, (t, a, b) in enumerate(parts)]
+        return [("s", t, a, m) for t, a, m, b in cut if m > a] + [("v", t, m, b) for t, a, m, b in cut if b > m]
+
+    def gather(q, t, c0, c1):
+        wait(q, "v", osa[t])
+        est[q] += CALL + GATHER * (c1 - c0)
+        return copy(q, T.xg[:, 4 * c0 + t:4 * c1:4], T.xs[:, 0:4 * NODES].indirect(T.osa[:, S1W * t + c0 // 16:S1W * t + c1 // 16]))
+
     free = {}
-    taken = {"v": 0, "s": 0}
-    half = [0]
+    bank = [0]
 
-    def multiply(road, h, own):
-        if road is None:
-            cb, pb, c0, w, o0 = "xoc", "xos", 0, NODES, 0
-            wait("t", "v", own)
+    def product(wc, wp, cb, pb, c0, w):
+        n = -(-w // BANK)
+        if bank[0] + n > BANKS:
+            bank[0] = 0
+        used = list(range(bank[0], bank[0] + n))
+        bank[0] += n
+        for j, b in enumerate(used):
+            a, e = c0 + BANK * j, c0 + min(w, BANK * (j + 1))
+            after("t", free.get(b, {}))
+            m = done(t_.matmul_mx(T.pp[:, BANK * b:BANK * b + e - a], wc, wp, T[cb][:, a:e], T[pb][:, a:e], True, True), "t")
+        return T.pp[:, BANK * used[0]:BANK * used[0] + w], m, used
+
+    table = {i: {"v": const} for i in range(4)}
+    ready = {}
+
+    comes = []
+    for road, a in came.items():
+        for k, r in enumerate(ranks[a]):
+            if r != rank:
+                h = [j for j in firsts(k, len(ranks[me])) if ranks[me][j] != r].index(mine)
+                calls = [len(beside(call, u)) for step in SENDS[k] for call in step[:2] for u in call if u[:2] == (road, h)]
+                count = sum(writer(road, k) // (j if road in (DIRECT, OWN) else 1) for j in calls)
+                comes.append((ARRIVE[mine].index((road, h)), road, NODES + r * C1, C1, {"x%d" % r: count}))
+    comes = [c[2:] for c in sorted(comes, key=lambda c: c[:2])]
+
+    def merged(blocks):
+        out = []
+        for c0, w, marks in blocks:
+            for o in out:
+                if (o[0] - NODES) // (2 * C1) == (c0 - NODES) // (2 * C1):
+                    out.remove(o)
+                    c0, w, marks = min(c0, o[0]), w + o[1], {**marks, **o[2]}
+                    break
+            out.append((c0, w, marks))
+        return out
+
+    def take(i, block, q=None):
+        c0, w, marks = block
+        q = q or min("sv", key=lambda k: est[k])
+        est[q] += CALL + EMPTY * w
+        after("t", ready["weights"])
+        after("t", marks)
+        z, m, used = product(T.w1c[:, 128 * i:128 * i + 128], T.w1p[:, 128 * i:128 * i + 128], "xc", "xp", c0, w)
+        wait(q, "t", m)
+        out = T["tb%d" % i][:, c0:c0 + w]
+        if q == "v":
+            table[i][q] = done(v_.tensor_scalar(out, z, 0.0, 0.05, A.max, A.mult), "v")
         else:
-            ks = [k for k in firsts(mine, len(ranks[came[road]])) if ranks[came[road]][k] != rank]
-            r = ranks[came[road]][ks[h]]
-            cb, pb, c0, w, o0 = "xrc", "xrs", r * C1, C1, NODES + r * C1
-            wait("t", "x%d" % r, 2 * writer(road, ks[h]))
-        banks = [512 * (half[0] + i) for i in range(4)]
-        half[0] = 4 - half[0]
-        mm = []
-        for i, bank in enumerate(banks):
-            if bank in free:
-                wait("t", *free[bank])
-            mm.append(done(t_.matmul_mx(T.pp[:, bank:bank + w], T.w1c[:, 128 * i:128 * i + 128], T.w1p[:, 128 * i:128 * i + 128],
-                                        T[cb][:, c0:c0 + w], T[pb][:, c0:c0 + w], True, True), "t"))
-        for i, bank in enumerate(banks):
-            q = "s" if est["s"] <= est["v"] else "v"
-            est[q] += 50 + 1.05 * w
-            wait(q, "t", mm[i])
-            out, z = T["tb%d" % i][:, o0:o0 + w], T.pp[:, bank:bank + w]
-            if q == "v":
-                taken[q] = done(v_.tensor_scalar(out, z, 0.0, 0.05, A.max, A.mult), "v")
-            else:
-                taken[q] = done(s_.activation(out, z, F.Relu, scale=0.05), "s")
-            free[bank] = (q, taken[q])
+            table[i][q] = done(s_.activation(out, z, F.Relu, scale=0.05), "s")
+        for b in used:
+            free[b] = {q: table[i][q]}
 
-    sent = 0
-    own = lists = 0
-    held = []
+    def source(i, e, a, b):
+        return T["tb%d" % i][:, 0:W].indirect(T.ore[:, EW * e + a // 16:EW * e + b // 16])
+
+    def pick(i, q, *ways):
+        after(q, most[i])
+        win, off = (T["r%d" % i][:, 0:NODES], OSB) if i in FOLDED else (T["r%d" % i][:, 0:4 * NODES], OSC)
+        for a, b in join([(r * C2, (r + 1) * C2) for road in ways or goes for r in ranks[goes[road]] if r != rank]):
+            picked[q] = copy(q, T.hg[:, 4 * a + i:4 * b:4], win.indirect(T.ore[:, off + a // 16:off + b // 16]))
+
+    def every(i, q, a, b):
+        after(q, lists)
+        after(q, table[i])
+        side[i, a] = {q: copy(q, T["gg%d" % i][:, 4 * a:4 * b], T["tb%d" % i][:, 0:W].indirect(T.ore[:, ORA + a // 4:ORA + b // 4]))}
+
+    def scan(i, a, b):
+        after("v", side[i, a])
+        most[i] = {"v": done(v_.tensor_tensor_scan(T["r%d" % i][:, 4 * a:4 * b], T.mk[:, 0:4 * (b - a)], T["gg%d" % i][:, 4 * a:4 * b],
+                                                   0.0, A.mult, A.max), "v")}
+
+    def first(i, q, a, b):
+        after(q, lists)
+        after(q, table[i])
+        most[i][q] = copy(q, T["gg%d" % i][:, a:b], source(i, 0, a, b))
+
+    def fold(i, e):
+        after("v", table[i])
+        after("v", most[i])
+        out = T["gg%d" % i][:, NODES * e:NODES * (e + 1)] if e < 3 else T["r%d" % i][:, 0:NODES]
+        most[i] = {"v": done(v_.tensor_tensor(out, source(i, e, 0, NODES), T["gg%d" % i][:, NODES * (e - 1):NODES * e], A.max), "v")}
+
+    sent = [0]
+    most, picked, side = {i: {} for i in range(4)}, {}, {}
+
+    def finish(items, calls, got):
+        after("v", got)
+        for item in items:
+            a, b = item[4], item[4] + item[5]
+            est["v"] += PACK * 4 * (b - a)
+            qd = done(v_.quantize_mx(T.xsc[:, a:b], T.xss[:, a:b], T.xg[:, 4 * a:4 * b]), "v")
+        for m, call in enumerate(calls):
+            if call:
+                wait("g", "v", qd)
+                sent[0] += send([unit(call, u) for u in call], "xsc", "xss", (m,))
+        if calls == SENDS[mine][LISTS][:2]:
+            other_lists()
+            est["v"] += SORT
+
     wait("v", "dx", 16)
     wait("s", "dx", 16)
-    for what, road, h in PLAN:
-        if what in ("send", "hold"):
-            item = unit(road, h)
-            held.append(item)
-            qd = gather(item[4], item[4] + item[5])
-            if what == "send":
-                wait("g", "v", qd)
-                sent += send(held, "xsc", "xss")
-                held = []
-        elif what == "take":
-            multiply(road, h, own)
-        elif what == "self":
+    held, blocks = [], []
+    for n, (codes, scales, *made) in enumerate(SENDS[mine]):
+        items, got = [unit([u], u) for u in (made or codes)], {}
+        owed = PACK * 4 * (sum(x[5] for y in held for x in y[0]) + NODES * ((n == WEIGHTS) + (n == MINE))) + SORT * (n == LISTS + 1)
+        for piece in pieces([(x[4], x[4] + x[5]) for x in items], owed - SOLO * (n == len(SENDS[mine]) - 1)):
+            got[piece[0]] = gather(*piece)
+            if piece[0] == "v" and held:
+                finish(*held.pop())
+        held.append((items, (codes, scales), got))
+        if n == WEIGHTS:
             wait("v", "dw1", 16)
-            done(v_.quantize_mx(T.w1c[:, :], T.w1p[:, :], T.w1s[:, :]), "v")
-            own = done(v_.quantize_mx(T.xoc[:, :], T.xos[:, :], T.xs[:, :]), "v")
-            est["v"] += 1150
-        elif what == "rows":
-            wait("v", "dra", 128)
-            wait("v", "drb", 16)
-            for b in range(4):
-                done(v_.tensor_copy(T.ecol[0:16, EW * b:EW * b + E1], T.lra[0:16, b:R1W:4]), "v")
-                ec = done(v_.tensor_copy(T.ecol[0:16, EW * b + E1:EW * (b + 1)], T.lrb[0:16, b:R2W:4]), "v")
-            est["v"] += 560
-            wait("y", "v", ec)
-            for e in range(4):
-                for b in range(4):
-                    g.sync.dma_start(T.erow[4 * b:4 * b + 4, EW * e:EW * (e + 1)],
-                                     T.ecol[e:16:4, EW * b:EW * (b + 1)]).then_inc(T.sem.der, 16)
-            g.sync.wait_ge(T.sem.der, 256)
-            load_list(g.sync, "ore", "erow", "dre", range(8))
-        else:
-            wait("v", "dw2", 16)
-            done(v_.quantize_mx(T.w2c[:, :], T.w2p[:, :], T.w2s[:, :]), "v")
-            done(v_.tensor_copy(T.ora[:, :], T.lra[:, :]), "v")
-            wait("v", "dsb", 128)
-            done(v_.tensor_copy(T.osb[:, :], T.lsb[:, :]), "v")
-            lists = done(v_.tensor_scalar(T.osc[:, :], T.lsb[:, :], 4, 3, A.mult, A.add), "v")
-            est["v"] += 450
+            est["v"] += PACK * 4 * NODES
+            ready["weights"] = {"v": done(v_.quantize_mx(T.w1c[:, :], T.w1p[:, :], T.w1s[:, :]), "v")}
+        if n == MINE:
+            est["v"] += PACK * 4 * NODES
+            blocks.append((0, NODES, {"v": done(v_.quantize_mx(T.xc[:, 0:NODES], T.xp[:, 0:NODES], T.xs[:, :]), "v")}))
+            blocks += comes
+        if n in NOLAG:
+            finish(*held.pop())
+        for _ in range(TAKE.count(n)):
+            block = blocks.pop(0)
+            for i in range(4):
+                take(i, block)
 
-    for q in "vs":
-        wait(q, "dre", 128)
-        wait(q, "v", max(taken["v"], lists, const))
-        wait(q, "s", taken["s"])
-    first = [(T["gg%d" % i][:, 0:NODES], T["tb%d" % i][:, 0:W].indirect(T.ore[:, 0:E1])) for i in (0, 1)]
-    acc = {0: ("s", done(s_.activation(*first[0], F.Copy), "s")), 1: ("v", done(v_.tensor_copy(*first[1]), "v"))}
-    pieces = {2: [(0, R1W)], 3: [(0, R1W // 2), (R1W // 2, 3 * R1W // 4), (3 * R1W // 4, R1W)]}
-    gs = {}
-    for i in (2, 3):
-        for a, b in pieces[i]:
-            gs[i, a] = done(s_.activation(T["gg%d" % i][:, 16 * a:16 * b], T["tb%d" % i][:, 0:W].indirect(T.ora[:, a:b]), F.Copy), "s")
-    for e in (1, 2, 3):
-        for i in (0, 1):
-            wait("v", *acc[i])
-            out = T["gg%d" % i][:, NODES * e:NODES * (e + 1)] if e < 3 else T["r%d" % i][:, :]
-            acc[i] = ("v", done(v_.tensor_tensor(out, T["tb%d" % i][:, 0:W].indirect(T.ore[:, EW * e:EW * e + E1]),
-                                                 T["gg%d" % i][:, NODES * (e - 1):NODES * e], A.max), "v"))
-    rd = {0: acc[0][1], 1: acc[1][1]}
-    for i in (2, 3):
-        for a, b in pieces[i]:
-            wait("v", "s", gs[i, a])
-            a, b = 16 * a, 16 * b
-            rd[i] = done(v_.tensor_tensor_scan(T["sc%d" % i][:, a:b], T.mk[:, a:b], T["gg%d" % i][:, a:b], 0.0, A.mult, A.max), "v")
+    for n, block in enumerate(blocks):
+        for i in (2, 0, 3, 1):
+            if n < len(blocks) - LATE[i]:
+                take(i, block, LAST.get(i) if n == len(blocks) - 1 else None)
 
-    for pair, whose in (((MATE, DIE), ("ss", "ss", "sv", "vv")), ((DIRECT, OWN), ("ss", "ss", "vv", "vv"))):
+    def rest(i, qs):
+        for n, block in enumerate(merged(blocks[len(blocks) - LATE[i]:])):
+            take(i, block, qs[n % len(qs)])
+
+    steps = {"first": first, "fold": fold, "all": every, "scan": scan, "pick": pick, "rest": rest}
+    for what, *how in MAXIMA:
+        steps[what](*how)
+
+    for pair, whose in zip(((MATE, DIE), (DIRECT, OWN)), PICKS):
         items = []
         for road in pair:
             to = takes(road)
-            eng = send_engines(core, to[0][2], T, topo)
+            eng = send_engines(core, to[0][2][0], T, topo)
             if road in (MATE, DIE):
-                items.append((to[0][2], ("f2c", "f2s"), 0, ("fc2", "fs2"), ranks[goes[road]][0] * C2, len(to) * C2, eng))
+                items.append((to[0][2], ("f2c", "f2s"), 0, "f2", ranks[goes[road]][0] * C2, len(to) * C2, eng))
                 continue
             e = len(eng) // len(to)
-            for n, (k, r, c) in enumerate(to):
+            for n, (k, r, cs) in enumerate(to):
                 bufs, at = (("hrc", "hrs"), rank * C2) if road == DIRECT else (("hoc", "hos"), NODES)
-                items.append((c, bufs, at, ("h%d" % rank,) * 2, r * C2, C2, eng[e * n:e * n + e]))
+                items.append((cs, bufs, at, "h%d" % rank, r * C2, C2, eng[e * n:e * n + e]))
         cols = [(ranks[goes[road]][0] * C2, (ranks[goes[road]][-1] + 1) * C2) for road in pair]
-        last = {}
-        for t in range(4):
-            for q in "sv":
-                for a, b in join([c for c, w in zip(cols, whose[t]) if w == q]):
-                    wait(q, "v", max(rd[t], lists))
-                    last[q] = pick(q, "hg", 2, t, a, b)
-        wait("v", "v", last["v"])
-        wait("v", "s", last["s"])
-        qd = quantise("hg", join(cols), "hsc", "hss")
+        for how in whose:
+            pick(*how)
+        after("v", picked)
+        for a, b in join(cols):
+            qd = done(v_.quantize_mx(T.hsc[:, a:b], T.hss[:, a:b], T.hg[:, 4 * a:4 * b]), "v")
         wait("g", "v", qd)
-        sent += send(items, "hsc", "hss")
-    for i in (0, 1):
-        hs = done(s_.activation(T.ht[:, i:4 * NODES:4], T["r%d" % i][:, :], F.Copy), "s")
-    for i in (2, 3):
-        hv = done(v_.tensor_copy(T.ht[:, i:4 * NODES:4], T["sc%d" % i][:, 3:4 * NODES:4]), "v")
-    wait("v", "v", hv)
-    wait("v", "s", hs)
-    qh = done(v_.quantize_mx(T.hoc[:, 0:NODES], T.hos[:, 0:NODES], T.ht[:, :]), "v")
+        sent[0] += send(items, "hsc", "hss")
+    whole = {}
+    for i in range(4):
+        q = WHOLE[i]
+        after(q, most[i])
+        whole[q] = copy(q, T.ht[:, i:4 * NODES:4], T["r%d" % i][:, 0:NODES] if i in FOLDED else T["r%d" % i][:, 3:4 * NODES:4])
+    wait("v", "dw2", 16)
+    done(v_.quantize_mx(T.w2c[:, :], T.w2p[:, :], T.w2s[:, :]), "v")
+    after("v", whole)
+    hn = NODES // 2
+    qh = [done(v_.quantize_mx(T.hoc[:, a:a + hn], T.hos[:, a:a + hn], T.ht[:, 4 * a:4 * (a + hn)]), "v") for a in (0, hn)]
 
-    blocks = [("hoc", "hos", 0, NODES, 0, 0, []),
+    blocks = [("hoc", "hos", 0, hn, 0, 0, [("v", qh[0])]), ("hoc", "hos", hn, hn, 0, hn, [("v", qh[1])]),
               ("hoc", "hos", NODES + C2 - 128, 128, 128 - C2, NODES + near[0] * C2, [("h%d" % near[0], 2 * writer(OWN, 1 - mine))])]
     for road in (DIRECT, DIE, MATE):
         rs = ranks[came[road]]
         sems = [("h%d" % r, 2 * writer(road, k) // len(ranks[me])) for k, r in enumerate(rs)]
         blocks.append(("hrc", "hrs", rs[0] * C2, len(rs) * C2, 0, NODES + rs[0] * C2, sems))
-    wait("t", "v", qh)
-    wait("t", "s", taken["s"])
-    uq = {"v": 0, "s": 0}
+    uq = {}
     for n, (cb, pb, c0, w, skip, o0, sems) in enumerate(blocks):
         for sem, val in sems:
             wait("t", sem, val)
-        m = done(t_.matmul_mx(T.pp[:, 512 * n:512 * n + w], T.w2c[:, :], T.w2p[:, :], T[cb][:, c0:c0 + w], T[pb][:, c0:c0 + w],
-                              True, True), "t")
-        out, z = T.ut[:, o0:o0 + w - skip], T.pp[:, 512 * n + skip:512 * n + w]
-        q = "sv"[n % 2]
+        z, m, used = product(T.w2c[:, :], T.w2p[:, :], cb, pb, c0, w)
+        q = EMPTIES[n]
         wait(q, "t", m)
-        uq[q] = done(s_.activation(out, z, F.Copy), "s") if q == "s" else done(v_.tensor_copy(out, z), "v")
+        uq[q] = copy(q, T.ut[:, o0:o0 + w - skip], T.pp[:, BANK * used[0] + skip:BANK * used[0] + w])
 
     for q in "sv":
-        wait(q, "v", uq["v"])
-        wait(q, "s", uq["s"])
+        after(q, uq)
 
-    def source(e, k):
+    def source2(e, k):
         return T.ut[:, 0:U].indirect(T.ore[:, EW * e + E1 + E2 // 2 * k:EW * e + E1 + E2 // 2 * (k + 1)])
 
     hw = TARGETS // 2
-    up = [("s", done(s_.activation(T.g2[:, hw * k:hw * (k + 1)], source(0, k), F.Copy), "s")) for k in (0, 1)]
+    up = [(q, copy(q, T.g2[:, hw * k:hw * (k + 1)], source2(0, k))) for k, q in enumerate(LEAD)]
     for e in (1, 2, 3):
         for k in (0, 1):
             wait("v", *up[k])
             out = T.g2[:, TARGETS * e + hw * k:TARGETS * e + hw * (k + 1)] if e < 3 else T.yo[:, hw * k:hw * (k + 1)]
-            up[k] = ("v", done(v_.tensor_tensor(out, source(e, k), T.g2[:, TARGETS * (e - 1) + hw * k:TARGETS * (e - 1) + hw * (k + 1)],
+            up[k] = ("v", done(v_.tensor_tensor(out, source2(e, k), T.g2[:, TARGETS * (e - 1) + hw * k:TARGETS * (e - 1) + hw * (k + 1)],
                                                 A.max), "v"))
     for k in (0, 1):
         wait("y", *up[k])
@@ -454,4 +505,4 @@ def rank_program(g, core, T, topo):
     for q in "vst":
         wait("y", q, cnt[q])
     g.sync.wait_ge(T.sem.dy, 32)
-    g.wait_ge(T.sem.loc, sent)
+    g.wait_ge(T.sem.loc, sent[0])

from concourse.bass import DstId, RemoteDMATransfer
from concourse.mybir import dt, AluOpType, ActivationFunctionType

N = 8
SIM_CORES = 128
NODES, TARGETS, C1, C2 = 512, 256, 320, 64
W = NODES + N * C1
U = NODES + N * C2
S1W, S2W = N * C1 // 16, N * C2 // 16
R1W, R2W = 4 * NODES // 16, 4 * TARGETS // 16
E1, E2 = NODES // 16, TARGETS // 16
EW = E1 + E2
ORA, OSB, OSC, OW = 4 * EW, 4 * EW + R1W, 4 * EW + R1W + S2W, 4 * EW + R1W + 2 * S2W
BANK, BANKS = 512, 8
MXC, MXS = "float8_e4m3fn_x4", "uint8"

SCRATCH = {
    "xs": ("sbuf", [128, 4 * NODES], "bfloat16"),
    "w1s": ("sbuf", [128, 4 * 512], "bfloat16"),
    "w2s": ("sbuf", [128, 4 * 128], "bfloat16"),
    "lsa": ("sbuf", [128, S1W], "int32"),
    "osa": ("sbuf", [128, 4 * S1W], "uint16"),
    "lr": ("sbuf", [16, 5, 4 * EW + 4], "int32"),
    "ore": ("sbuf", [128, OW], "uint16"),
    "xg": ("sbuf", [128, 4 * N * C1], "bfloat16"),
    "xsc": ("sbuf", [128, N * C1], MXC), "xss": ("sbuf", [128, N * C1], MXS),
    "xc": ("sbuf", [128, W], MXC), "xp": ("sbuf", [128, W], MXS),
    "w1c": ("sbuf", [128, 512], MXC), "w1p": ("sbuf", [128, 512], MXS),
    "w2c": ("sbuf", [128, 128], MXC), "w2p": ("sbuf", [128, 128], MXS),
    "tb0": ("sbuf", [128, W], "bfloat16"), "tb1": ("sbuf", [128, W], "bfloat16"),
    "tb2": ("sbuf", [128, W], "bfloat16"), "tb3": ("sbuf", [128, W], "bfloat16"),
    "gg0": ("sbuf", [128, 4 * NODES], "bfloat16"), "gg1": ("sbuf", [128, 4 * NODES], "bfloat16"),
    "gg2": ("sbuf", [128, 4 * NODES], "bfloat16"), "gg3": ("sbuf", [128, 4 * NODES], "bfloat16"),
    "r0": ("sbuf", [128, 4 * NODES], "bfloat16"), "r1": ("sbuf", [128, 4 * NODES], "bfloat16"),
    "r2": ("sbuf", [128, 4 * NODES], "bfloat16"), "r3": ("sbuf", [128, 4 * NODES], "bfloat16"),
    "mk": ("sbuf", [128, 2 * NODES], "bfloat16"),
    "ht": ("sbuf", [128, 4 * NODES], "bfloat16"),
    "hg": ("sbuf", [128, 4 * N * C2], "bfloat16"),
    "hsc": ("sbuf", [128, N * C2], MXC), "hss": ("sbuf", [128, N * C2], MXS),
    "hoc": ("sbuf", [128, NODES + C2], MXC), "hos": ("sbuf", [128, NODES + C2], MXS),
    "hrc": ("sbuf", [128, N * C2], MXC), "hrs": ("sbuf", [128, N * C2], MXS),
    "ut": ("sbuf", [128, U], "float32"),
    "g2": ("sbuf", [128, 3 * TARGETS], "float32"),
    "yo": ("sbuf", [128, TARGETS], "float32"),
    "f1c": ("sbuf", [128, 2 * C1], MXC), "f1s": ("sbuf", [128, 2 * C1], MXS),
    "f2c": ("sbuf", [128, 2 * C2], MXC), "f2s": ("sbuf", [128, 2 * C2], MXS),
    "pp": ("psum", [128, BANK * BANKS], "float32"),
}
SEMAPHORES = (["v", "s", "t", "loc", "dx", "dw1", "dw2", "dsa", "dr", "dre", "dy", "f100", "f101", "f110", "f111", "f2"]
              + ["x%d" % r for r in range(N)] + ["h%d" % r for r in range(N)])

MATE, DIE, DIRECT, OWN = "mate", "die", "direct", "own"

M0, M1, D0, D1, R0, R1, O0 = (MATE, 0), (MATE, 1), (DIE, 0), (DIE, 1), (DIRECT, 0), (DIRECT, 1), (OWN, 0)
SENDS = [(([M0], []), ([D0], [M0, D0]), ([R0], [R0]), ([M1], []), ([D1], [M1, D1]), ([R1], []), ([O0], [R1, O0])),
         (([D0], []), ([M0], [M0, D0]), ([R0], [R0]), ([D1], []), ([M1], [M1, D1]), ([R1], []), ([O0], [R1, O0]))]
NOLAG = (0, 6)
SOLO = 0
AHEAD, BEHIND, LISTS, LAG, SORT = 4, 0, 6, 0, 420
NEARBY = False
ARRIVE = [(R0, M0, D0, O0, D1, R1, M1), (R0, D0, M0, O0, M1, R1, D1)]
WEIGHTS, MINE, TAKE = 2, 3, (6,)
LATE = (0, 0, 0, 0)
FOLDED, LEAD, SNAP, EMPTIES, WHOLE = (0, 1), "vs", 96, "svsvsv", "ssvv"
PICKS = (((1, "s", MATE), (1, "v", DIE)),
         ((3, "s", DIRECT, OWN), (2, "s", DIRECT, OWN), (0, "v", DIRECT, OWN), (1, "v", DIRECT, OWN)))
LAST = {2: "s", 0: "v", 3: "s", 1: "v"}
MAXIMA = (("all", 2, "s", 0, 256), ("first", 0, "v", 0, 512), ("all", 2, "s", 256, 512), ("fold", 0, 1), ("scan", 2, 0, 256),
          ("first", 1, "s", 0, 384), ("first", 1, "v", 384, 512),
          ("fold", 0, 2), ("scan", 2, 256, 512), ("fold", 1, 1), ("fold", 0, 3),
          ("all", 3, "s", 0, 256), ("all", 3, "s", 256, 512), ("pick", 2, "s", MATE, DIE), ("pick", 0, "s", MATE, DIE),
          ("scan", 3, 0, 256), ("fold", 1, 2), ("scan", 3, 256, 512), ("fold", 1, 3), ("pick", 3, "s", MATE, DIE))
CALL, GATHER, EMPTY, PACK = 55, 1.4, 0.87, 0.23


def layout(T, topo):
    chips, ranks = [], {}
    for r, c in enumerate(T.cores):
        ch = topo.chip(c)
        if ch not in ranks:
            chips.append(ch)
            ranks[ch] = []
        ranks[ch].append(r)
    roads = {}
    for ia, a in enumerate(chips):
        for ib, b in enumerate(chips):
            if a == b:
                roads[a, b] = (OWN, None)
                continue
            src, dst = T.cores[ranks[a][0]], T.cores[ranks[b][0]]
            k = len(ranks[a])
            if topo.same_plane(a, b):
                mid = [c for c in topo.cores_of(src) if topo.may_write(c, dst) and T.rank_of(c) is None]
                far = [c for c in mid if topo.die(c) != topo.die(src)]
                roads[a, b] = (DIE, far[:k] + ([c for c in mid if c not in far][:k] if NEARBY else far[k:2 * k]))
            elif (ib - ia) % len(chips) == 1:
                roads[a, b] = (DIRECT, None)
            else:
                mid = [c for c in range(SIM_CORES) if topo.mates(topo.chip(c), b)
                       and topo.may_write(c, dst) and topo.may_write(src, c) and T.rank_of(c) is None]
                dies = [[c for c in mid if (topo.die(c) != topo.die(dst)) == far] for far in (False, True)]
                roads[a, b] = (MATE, [dies[(j + m) % 2][j] for m in range(2) for j in range(k)])
    return chips, ranks, roads


def bits(engines):
    m = 0
    for e in engines:
        m |= 1 << e
    return m


def u8(view):
    return view.bitcast(dt.uint8)


def firsts(k, n):
    return [(k + i) % n for i in range(n)]


def send_engines(src, dst, T, topo):
    e = topo.engines(src, dst)
    if topo.chip(src) != topo.chip(dst):
        return e
    far = [c for c in T.cores if topo.chip(c) != topo.chip(src)][0]
    off = topo.engines(src, far)
    return [k for k in e if k not in off]


def beside(call, u):
    return [x for x in call if (x[0] in (MATE, DIRECT)) == (u[0] in (MATE, DIRECT))]


def hand_on(g, core, T, topo):
    chips, ranks, roads = layout(T, topo)
    for (a, b), (road, mid) in roads.items():
        if not mid or core not in mid:
            continue
        m, k = divmod(mid.index(core), len(ranks[a]))
        view = (u8, lambda v: v)[m]
        s = ranks[a][k]
        n = len(ranks[b])
        w = len(send_engines(T.cores[s], core, T, topo))
        sent = 0
        for (h, c0, c1), j in [((u + (0, C1))[1:4], len(beside(step[m], u))) for step in SENDS[k] for u in step[m] if u[0] == road]:
            d = firsts(k, n)[h]
            dst = T.cores[ranks[b][d]]
            rid, pid, _ = topo.addr(dst)
            eng = topo.engines(core, dst)
            o, i = T[("xc", "xp")[m]][:, NODES + s * C1 + c0:NODES + s * C1 + c1], T[("f1c", "f1s")[m]][:, d * C1 + c0:d * C1 + c1]
            g.wait_ge(T.sem["f1%d%d" % (h, c1 < C1)], w // j)
            g.remote_dma(view(o), view(i), T.sem["x%d" % s], T.sem.loc, pid, rid, bits(eng))
            sent += len(eng)
        tr = []
        for d in range(n):
            dst = T.cores[ranks[b][d]]
            rid, pid, _ = topo.addr(dst)
            eng = topo.engines(core, dst)
            e = len(eng) // n
            o, i = T[("hrc", "hrs")[m]][:, s * C2:(s + 1) * C2], T[("f2c", "f2s")[m]][:, d * C2:(d + 1) * C2]
            tr.append(RemoteDMATransfer(dst_ids=[DstId(rid=rid, pnc=pid)], dma_engine_mask=bits(eng[e * d:e * d + e]),
                                        remote_sem=T.sem["h%d" % s], src=view(i), dst=view(o)))
            sent += e
        g.wait_ge(T.sem.f2, w)
        g.remote_dma_fused(tr, local_sem=T.sem.loc)
        g.wait_ge(T.sem.loc, sent)


def join(runs):
    out = []
    for a, b in sorted(runs):
        if out and out[-1][1] == a:
            out[-1] = (out[-1][0], b)
        else:
            out.append((a, b))
    return out


def rank_program(g, core, T, topo):
    rank = T.rank_of(core)
    if rank is None:
        hand_on(g, core, T, topo)
        return
    chips, ranks, roads = layout(T, topo)
    me = topo.chip(core)
    mine = ranks[me].index(rank)
    near = [r for r in ranks[me] if r != rank]
    goes = {roads[me, b][0]: b for b in chips}
    came = {roads[a, me][0]: a for a in chips}
    v_, s_, t_ = g.vector, g.scalar, g.tensor
    A, F = AluOpType, ActivationFunctionType
    cnt = {"v": 0, "s": 0, "t": 0}
    seen = {}
    queues = {"g": g, "v": v_, "s": s_, "t": t_, "y": g.sync}

    def done(ins, q):
        ins.then_inc(T.sem[q], 1)
        cnt[q] += 1
        return cnt[q]

    def wait(q, sem, val):
        if val > seen.get((q, sem), 0):
            seen[q, sem] = val
            queues[q].wait_ge(T.sem[sem], val)

    def after(q, marks):
        for sem, val in marks.items():
            wait(q, sem, val)

    def load_list(q, buf, src, sem, ks):
        for k in ks:
            q.dma_start(T[buf][16 * k:16 * k + 16, :], T[src][:, :]).then_inc(T.sem[sem], 16)

    load_list(s_, "lsa", "snd1", "dsa", range(0, AHEAD))
    s_.dma_start(T.xs[:, :], T.x[:, :]).then_inc(T.sem.dx, 16)
    load_list(s_, "lsa", "snd1", "dsa", range(AHEAD, AHEAD + BEHIND))
    load_list(g.sync, "lsa", "snd1", "dsa", range(AHEAD + BEHIND, 8))
    wait("y", "dsa", 128)
    g.sync.dma_start(T.w1s[:, :], T.w1[:, :]).then_inc(T.sem.dw1, 16)
    g.sync.dma_start(T.w2s[:, :], T.w2[:, :]).then_inc(T.sem.dw2, 16)
    for b in range(4):
        g.sync.dma_start(T.lr[4 * b:4 * b + 4, 0:4, 4 - b:4 - b + R1W], T.src1[:, :]).then_inc(T.sem.dr, 16)
        g.sync.dma_start(T.lr[4 * b:4 * b + 4, 0:4, 4 - b + R1W:4 - b + 4 * EW], T.src2[:, :]).then_inc(T.sem.dr, 16)
    g.sync.dma_start(T.lr[:, 4, 0:R1W], T.src1[:, :]).then_inc(T.sem.dr, 16)
    g.sync.dma_start(T.lr[:, 4, R1W:R1W + S2W], T.snd2[:, :]).then_inc(T.sem.dr, 16)

    for t in range(4):
        done(v_.memset(T.mk[:, t:2 * NODES:4], 1.0 if t else 0.0), "v")
    for i in range(4):
        done(v_.memset(T["tb%d" % i][:, NODES + rank * C1:NODES + (rank + 1) * C1], 0.0), "v")
    done(v_.memset(T.hg[:, 4 * rank * C2:4 * (rank + 1) * C2], 0.0), "v")
    const = done(v_.memset(T.ut[:, NODES + rank * C2:NODES + (rank + 1) * C2], 0.0), "v")

    wait("v", "dsa", 128)
    osa = {}
    for t in (2, 3, 0, 1):
        osa[t] = done(v_.tensor_scalar(T.osa[:, S1W * t:S1W * (t + 1)], T.lsa[:, :], 4, t, A.mult, A.add), "v")

    def other_lists():
        wait("v", "dr", 10 * 16)
        done(v_.tensor_copy(T.ore[0:16, 0:ORA], T.lr[:, 0:4, 4:4 + 4 * EW:4]), "v")
        done(v_.tensor_copy(T.ore[0:16, ORA:OSC], T.lr[:, 4, 0:R1W + S2W]), "v")
        wait("y", "v", done(v_.tensor_scalar(T.ore[0:16, OSC:OW], T.lr[:, 4, R1W:R1W + S2W], 4, 3, A.mult, A.add), "v"))
        for k in range(1, 8):
            g.sync.dma_start(T.ore[16 * k:16 * k + 16, :], T.ore[0:16, :]).then_inc(T.sem.dre, 16)

    lists = {"dre": 7 * 16}

    def copy(q, out, in_):
        return done(v_.tensor_copy(out, in_), "v") if q == "v" else done(s_.activation(out, in_, F.Copy), "s")

    def send(items, sc, ss, parts=(0, 1)):
        for m in parts:
            tr = []
            for cs, bufs, d0, sem, c0, n, eng in items:
                d, s = T[bufs[m]][:, d0:d0 + n], T[(sc, ss)[m]][:, c0:c0 + n]
                if m == 0:
                    d, s = u8(d), u8(s)
                rid, pid, _ = topo.addr(cs[m])
                tr.append(RemoteDMATransfer(dst_ids=[DstId(rid=rid, pnc=pid)], dma_engine_mask=bits(eng),
                                            remote_sem=T.sem[sem], src=s, dst=d))
            g.remote_dma_fused(tr, local_sem=T.sem.loc)
        return len(parts) * sum(len(x[6]) for x in items)

    def takes(road):
        b = goes[road]
        mid = roads[me, b][1]
        ks = [k for k in firsts(mine, len(ranks[b])) if ranks[b][k] != rank]
        return [(k, ranks[b][k], mid[mine::len(ranks[me])] if mid else [T.cores[ranks[b][k]]] * 2) for k in ks]

    def unit(call, u):
        road, h, a, b = (u + (0, C1))[:4]
        k, r, cs = takes(road)[h]
        eng, with_u = send_engines(core, cs[0], T, topo), beside(call, u)
        e = len(eng) // len(with_u)
        eng = eng[e * with_u.index(u):e * with_u.index(u) + e]
        if road in (MATE, DIE):
            return (cs, ("f1c", "f1s"), k * C1 + a, "f1%d%d" % (h, b < C1), r * C1 + a, b - a, eng)
        return (cs, ("xc", "xp"), NODES + rank * C1 + a, "x%d" % rank, r * C1 + a, b - a, eng)

    def writer(road, k):
        a = came[road]
        mid = roads[a, me][1]
        c = mid[k] if mid else T.cores[ranks[a][k]]
        return len(send_engines(c, core, T, topo)) if T.rank_of(c) is not None else len(topo.engines(c, core))

    est = {"v": LAG, "s": 0.0}

    def pieces(runs, owed):
        n, parts = runs[0][1] - runs[0][0], [(t, a, b) for t in (2, 3, 0, 1) for a, b in runs]
        k = min(n * len(parts), max(0, 32 * round((n * len(parts) + (est["v"] + owed - est["s"]) / GATHER) / 64)))
        k = min((k, n * round(k / n)), key=lambda m: abs(m - k) - (SNAP if m % n == 0 else 0))
        cut = [(t, a, a + min(n, max(0, k - j * n)), b) for j, (t, a, b) in enumerate(parts)]
        return [("s", t, a, m) for t, a, m, b in cut if m > a] + [("v", t, m, b) for t, a, m, b in cut if b > m]

    def gather(q, t, c0, c1):
        wait(q, "v", osa[t])
        est[q] += CALL + GATHER * (c1 - c0)
        return copy(q, T.xg[:, 4 * c0 + t:4 * c1:4], T.xs[:, 0:4 * NODES].indirect(T.osa[:, S1W * t + c0 // 16:S1W * t + c1 // 16]))

    free = {}
    bank = [0]

    def product(wc, wp, cb, pb, c0, w):
        n = -(-w // BANK)
        if bank[0] + n > BANKS:
            bank[0] = 0
        used = list(range(bank[0], bank[0] + n))
        bank[0] += n
        for j, b in enumerate(used):
            a, e = c0 + BANK * j, c0 + min(w, BANK * (j + 1))
            after("t", free.get(b, {}))
            m = done(t_.matmul_mx(T.pp[:, BANK * b:BANK * b + e - a], wc, wp, T[cb][:, a:e], T[pb][:, a:e], True, True), "t")
        return T.pp[:, BANK * used[0]:BANK * used[0] + w], m, used

    table = {i: {"v": const} for i in range(4)}
    ready = {}

    comes = []
    for road, a in came.items():
        for k, r in enumerate(ranks[a]):
            if r != rank:
                h = [j for j in firsts(k, len(ranks[me])) if ranks[me][j] != r].index(mine)
                calls = [len(beside(call, u)) for step in SENDS[k] for call in step[:2] for u in call if u[:2] == (road, h)]
                count = sum(writer(road, k) // (j if road in (DIRECT, OWN) else 1) for j in calls)
                comes.append((ARRIVE[mine].index((road, h)), road, NODES + r * C1, C1, {"x%d" % r: count}))
    comes = [c[2:] for c in sorted(comes, key=lambda c: c[:2])]

    def merged(blocks):
        out = []
        for c0, w, marks in blocks:
            for o in out:
                if (o[0] - NODES) // (2 * C1) == (c0 - NODES) // (2 * C1):
                    out.remove(o)
                    c0, w, marks = min(c0, o[0]), w + o[1], {**marks, **o[2]}
                    break
            out.append((c0, w, marks))
        return out

    def take(i, block, q=None):
        c0, w, marks = block
        q = q or min("sv", key=lambda k: est[k])
        est[q] += CALL + EMPTY * w
        after("t", ready["weights"])
        after("t", marks)
        z, m, used = product(T.w1c[:, 128 * i:128 * i + 128], T.w1p[:, 128 * i:128 * i + 128], "xc", "xp", c0, w)
        wait(q, "t", m)
        out = T["tb%d" % i][:, c0:c0 + w]
        if q == "v":
            table[i][q] = done(v_.tensor_scalar(out, z, 0.0, 0.05, A.max, A.mult), "v")
        else:
            table[i][q] = done(s_.activation(out, z, F.Relu, scale=0.05), "s")
        for b in used:
            free[b] = {q: table[i][q]}

    def source(i, e, a, b):
        return T["tb%d" % i][:, 0:W].indirect(T.ore[:, EW * e + a // 16:EW * e + b // 16])

    def pick(i, q, *ways):
        after(q, most[i])
        win, off = (T["r%d" % i][:, 0:NODES], OSB) if i in FOLDED else (T["r%d" % i][:, 0:4 * NODES], OSC)
        for a, b in join([(r * C2, (r + 1) * C2) for road in ways or goes for r in ranks[goes[road]] if r != rank]):
            picked[q] = copy(q, T.hg[:, 4 * a + i:4 * b:4], win.indirect(T.ore[:, off + a // 16:off + b // 16]))

    def every(i, q, a, b):
        after(q, lists)
        after(q, table[i])
        side[i, a] = {q: copy(q, T["gg%d" % i][:, 4 * a:4 * b], T["tb%d" % i][:, 0:W].indirect(T.ore[:, ORA + a // 4:ORA + b // 4]))}

    def scan(i, a, b):
        after("v", side[i, a])
        most[i] = {"v": done(v_.tensor_tensor_scan(T["r%d" % i][:, 4 * a:4 * b], T.mk[:, 0:4 * (b - a)], T["gg%d" % i][:, 4 * a:4 * b],
                                                   0.0, A.mult, A.max), "v")}

    def first(i, q, a, b):
        after(q, lists)
        after(q, table[i])
        most[i][q] = copy(q, T["gg%d" % i][:, a:b], source(i, 0, a, b))

    def fold(i, e):
        after("v", table[i])
        after("v", most[i])
        out = T["gg%d" % i][:, NODES * e:NODES * (e + 1)] if e < 3 else T["r%d" % i][:, 0:NODES]
        most[i] = {"v": done(v_.tensor_tensor(out, source(i, e, 0, NODES), T["gg%d" % i][:, NODES * (e - 1):NODES * e], A.max), "v")}

    sent = [0]
    most, picked, side = {i: {} for i in range(4)}, {}, {}

    def finish(items, calls, got):
        after("v", got)
        for item in items:
            a, b = item[4], item[4] + item[5]
            est["v"] += PACK * 4 * (b - a)
            qd = done(v_.quantize_mx(T.xsc[:, a:b], T.xss[:, a:b], T.xg[:, 4 * a:4 * b]), "v")
        for m, call in enumerate(calls):
            if call:
                wait("g", "v", qd)
                sent[0] += send([unit(call, u) for u in call], "xsc", "xss", (m,))
        if calls == SENDS[mine][LISTS][:2]:
            other_lists()
            est["v"] += SORT

    wait("v", "dx", 16)
    wait("s", "dx", 16)
    held, blocks = [], []
    for n, (codes, scales, *made) in enumerate(SENDS[mine]):
        items, got = [unit([u], u) for u in (made or codes)], {}
        owed = PACK * 4 * (sum(x[5] for y in held for x in y[0]) + NODES * ((n == WEIGHTS) + (n == MINE))) + SORT * (n == LISTS + 1)
        for piece in pieces([(x[4], x[4] + x[5]) for x in items], owed - SOLO * (n == len(SENDS[mine]) - 1)):
            got[piece[0]] = gather(*piece)
            if piece[0] == "v" and held:
                finish(*held.pop())
        held.append((items, (codes, scales), got))
        if n == WEIGHTS:
            wait("v", "dw1", 16)
            est["v"] += PACK * 4 * NODES
            ready["weights"] = {"v": done(v_.quantize_mx(T.w1c[:, :], T.w1p[:, :], T.w1s[:, :]), "v")}
        if n == MINE:
            est["v"] += PACK * 4 * NODES
            blocks.append((0, NODES, {"v": done(v_.quantize_mx(T.xc[:, 0:NODES], T.xp[:, 0:NODES], T.xs[:, :]), "v")}))
            blocks += comes
        if n in NOLAG:
            finish(*held.pop())
        for _ in range(TAKE.count(n)):
            block = blocks.pop(0)
            for i in range(4):
                take(i, block)

    for n, block in enumerate(blocks):
        for i in (2, 0, 3, 1):
            if n < len(blocks) - LATE[i]:
                take(i, block, LAST.get(i) if n == len(blocks) - 1 else None)

    def rest(i, qs):
        for n, block in enumerate(merged(blocks[len(blocks) - LATE[i]:])):
            take(i, block, qs[n % len(qs)])

    steps = {"first": first, "fold": fold, "all": every, "scan": scan, "pick": pick, "rest": rest}
    for what, *how in MAXIMA:
        steps[what](*how)

    for pair, whose in zip(((MATE, DIE), (DIRECT, OWN)), PICKS):
        items = []
        for road in pair:
            to = takes(road)
            eng = send_engines(core, to[0][2][0], T, topo)
            if road in (MATE, DIE):
                items.append((to[0][2], ("f2c", "f2s"), 0, "f2", ranks[goes[road]][0] * C2, len(to) * C2, eng))
                continue
            e = len(eng) // len(to)
            for n, (k, r, cs) in enumerate(to):
                bufs, at = (("hrc", "hrs"), rank * C2) if road == DIRECT else (("hoc", "hos"), NODES)
                items.append((cs, bufs, at, "h%d" % rank, r * C2, C2, eng[e * n:e * n + e]))
        cols = [(ranks[goes[road]][0] * C2, (ranks[goes[road]][-1] + 1) * C2) for road in pair]
        for how in whose:
            pick(*how)
        after("v", picked)
        for a, b in join(cols):
            qd = done(v_.quantize_mx(T.hsc[:, a:b], T.hss[:, a:b], T.hg[:, 4 * a:4 * b]), "v")
        wait("g", "v", qd)
        sent[0] += send(items, "hsc", "hss")
    whole = {}
    for i in range(4):
        q = WHOLE[i]
        after(q, most[i])
        whole[q] = copy(q, T.ht[:, i:4 * NODES:4], T["r%d" % i][:, 0:NODES] if i in FOLDED else T["r%d" % i][:, 3:4 * NODES:4])
    wait("v", "dw2", 16)
    done(v_.quantize_mx(T.w2c[:, :], T.w2p[:, :], T.w2s[:, :]), "v")
    after("v", whole)
    hn = NODES // 2
    qh = [done(v_.quantize_mx(T.hoc[:, a:a + hn], T.hos[:, a:a + hn], T.ht[:, 4 * a:4 * (a + hn)]), "v") for a in (0, hn)]

    blocks = [("hoc", "hos", 0, hn, 0, 0, [("v", qh[0])]), ("hoc", "hos", hn, hn, 0, hn, [("v", qh[1])]),
              ("hoc", "hos", NODES + C2 - 128, 128, 128 - C2, NODES + near[0] * C2, [("h%d" % near[0], 2 * writer(OWN, 1 - mine))])]
    for road in (DIRECT, DIE, MATE):
        rs = ranks[came[road]]
        sems = [("h%d" % r, 2 * writer(road, k) // len(ranks[me])) for k, r in enumerate(rs)]
        blocks.append(("hrc", "hrs", rs[0] * C2, len(rs) * C2, 0, NODES + rs[0] * C2, sems))
    uq = {}
    for n, (cb, pb, c0, w, skip, o0, sems) in enumerate(blocks):
        for sem, val in sems:
            wait("t", sem, val)
        z, m, used = product(T.w2c[:, :], T.w2p[:, :], cb, pb, c0, w)
        q = EMPTIES[n]
        wait(q, "t", m)
        uq[q] = copy(q, T.ut[:, o0:o0 + w - skip], T.pp[:, BANK * used[0] + skip:BANK * used[0] + w])

    for q in "sv":
        after(q, uq)

    def source2(e, k):
        return T.ut[:, 0:U].indirect(T.ore[:, EW * e + E1 + E2 // 2 * k:EW * e + E1 + E2 // 2 * (k + 1)])

    hw = TARGETS // 2
    up = [(q, copy(q, T.g2[:, hw * k:hw * (k + 1)], source2(0, k))) for k, q in enumerate(LEAD)]
    for e in (1, 2, 3):
        for k in (0, 1):
            wait("v", *up[k])
            out = T.g2[:, TARGETS * e + hw * k:TARGETS * e + hw * (k + 1)] if e < 3 else T.yo[:, hw * k:hw * (k + 1)]
            up[k] = ("v", done(v_.tensor_tensor(out, source2(e, k), T.g2[:, TARGETS * (e - 1) + hw * k:TARGETS * (e - 1) + hw * (k + 1)],
                                                A.max), "v"))
    for k in (0, 1):
        wait("y", *up[k])
        g.sync.dma_start(T.y[:, hw * k:hw * (k + 1)], T.yo[:, hw * k:hw * (k + 1)]).then_inc(T.sem.dy, 16)
    for q in "vst":
        wait("y", q, cnt[q])
    g.sync.wait_ge(T.sem.dy, 32)
    g.wait_ge(T.sem.loc, sent[0])
